import numpy as np, ml_dtypes
CORES = [2,3,42,43,82,83,122,123]
N = 8
import mx_ref
BF = ml_dtypes.bfloat16
def entries(a):
    return np.ascontiguousarray(a.T).reshape(-1)
def table(e):
    return np.ascontiguousarray(np.reshape(e, (-1, 16)).T).astype(np.int32)
def cols(t, e):
    v = np.concatenate([t.reshape(128, -1, 4), np.zeros((128, 1, 4), BF)], axis=1)
    return np.ascontiguousarray(v[:, e]).reshape(128, -1)
def f(rng, *shape):
    return mx_ref.flush((rng.standard_normal(shape, dtype=np.float32) * np.exp2(rng.integers(-2, 3, shape[:-1] + (1,)))).astype(BF))
def wide(rng, *shape, cols=0):
    v = rng.standard_normal(shape, dtype=np.float32) * np.exp2(rng.integers(-12, 13, shape)).astype(np.float32)
    if cols: v *= np.repeat(np.exp2(rng.integers(-cols, cols + 1, shape[:-2] + (1, shape[-1] // 4))) * (rng.random(shape[:-2] + (1, shape[-1] // 4)) > 0.0625), 4, axis=-1).astype(np.float32)
    return mx_ref.flush(v.astype(BF))
T, CAPP = 512, 96
def lists(rng, full=False, skew=False, single=False, back=False):
    if full:
        v = rng.permutation(([CAPP] * (T // CAPP) + [T % CAPP] + [0] * N)[:N])
        n = v[(np.arange(N)[None, :] - np.arange(N)[:, None]) % N][rng.permutation(N)][:, rng.permutation(N)]
    else:
        n = np.full((N, N), T // N)
        for _ in range(20 * N):
            (s, t), (d, e) = rng.permutation(N)[:2], rng.permutation(N)[:2]
            k = rng.integers(0, min(n[s, d], n[t, e], CAPP - n[s, e], CAPP - n[t, d]) + 1)
            n[s, d] -= k; n[t, e] -= k; n[s, e] += k; n[t, d] += k
    a = np.full((N, N * CAPP), -1)
    for s in range(N):
        parts = np.split(rng.permutation(T), np.cumsum(n[s])[:-1])
        for d in range(N): a[s, d * CAPP + rng.permutation(CAPP)[:n[s, d]]] = parts[d]
    p, u, o = [], [], []
    for r in range(N):
        used = np.flatnonzero(a[:, r * CAPP:(r + 1) * CAPP].reshape(-1) >= 0)
        p.append(table(used[::-1] if back else rng.permutation(used)))
        h = rng.integers(0, N)
        c = rng.integers(0, 2, N) if full else (np.full(N, -1) if rng.random() < 0.5 else rng.integers(0, 2, N)) if single else rng.integers(-1, 2, N)
        if c[h] < 0: c[h] = rng.integers(0, 2)
        named = np.flatnonzero(c >= 0)
        if single: named = np.array([h])
        if skew:
            m = rng.integers(T // 2 + 1, T + 1)
            e = np.sort(np.concatenate([np.full(m, h), rng.choice(named, T - m)]))
        elif full: e = np.sort(np.concatenate([named, rng.choice(named, T - N)]))
        else: e = np.repeat(named, np.diff(np.concatenate([[0], np.sort(rng.integers(0, T + 1, len(named) - 1)), [T]])))
        u.append(table(np.concatenate([c, np.full(16 - N, -1)]))); o.append(table(e))
    return {"send": np.stack([table(k) for k in a]), "place": np.stack(p), "sel": np.stack(u), "of": np.stack(o)}
def setup_inputs(rng):
    return {"x": f(rng, N, 128, 4 * T), "w": f(rng, N, 256, 512), **lists(rng)}
def setup_inputs_full(rng):
    return {**setup_inputs(rng), **lists(rng, full=True)}
def setup_inputs_reversed(rng):
    return {**setup_inputs(rng), **lists(rng, back=True)}
def setup_inputs_single(rng):
    return {**setup_inputs(rng), **lists(rng, single=True)}
def setup_inputs_skew(rng):
    return {**setup_inputs(rng), **lists(rng, skew=True)}
def setup_inputs_spread(rng):
    d = setup_inputs(rng); d["x"] = wide(rng, N, 128, 4 * T, cols=8); return d
def check_inputs(d):
    b = []
    for k in ("x", "w"):
        a = np.abs(d[k].astype(np.float32))
        if not ((a == 0) | ((a >= 2.0 ** -30) & (a <= 2.0 ** 30))).all(): b.append(k)
    sends = np.stack([entries(d["send"][r]) for r in range(N)])
    for r in range(N):
        c, p, u, e = sends[r], entries(d["place"][r]), entries(d["sel"][r]), entries(d["of"][r])
        if c.min() < -1 or not np.array_equal(np.sort(c[c >= 0]), np.arange(T)): b.append("send")
        if not np.array_equal(np.sort(p), np.flatnonzero(sends[:, r * CAPP:(r + 1) * CAPP].reshape(-1) >= 0)): b.append("place")
        if u.min() < -1 or u.max() > 1 or (u[N:] != -1).any(): b.append("sel")
        if e.min() < 0 or e.max() >= N or (np.diff(e) < 0).any() or (u[e] < 0).any(): b.append("of")
    return b
def reference(x, w, send, place, sel, of):
    W = [[mx_ref.quantize(w[h][128 * m:128 * m + 128]) for m in range(2)] for h in range(N)]
    y = np.zeros((N, 128, T), np.float32)
    for r in range(N):
        slots = np.concatenate([cols(x[s], entries(send[s])[r * CAPP:(r + 1) * CAPP]) for s in range(N)], axis=1)
        X = mx_ref.quantize(cols(slots, entries(place[r])))
        u, e = entries(sel[r]), entries(of[r])
        for h in range(N):
            i = e == h
            if i.any(): y[r][:, i] = mx_ref.matmul(W[h][u[h]], X)[:, i]
    return {"y": y}

@@ -1,0 +1,256 @@
+from concourse.bass import DstId, RemoteDMATransfer
+from concourse.mybir import dt, AluOpType, ActivationFunctionType
+
+N, TC, CAPP, NE = 8, 512, 96, 128
+SLOTS = N * CAPP
+HALF = SLOTS // 2
+CODE = "float8_e4m3fn_x4"
+
+
+def sb(n, t, p=128):
+    return ("sbuf", [p, n], t)
+
+
+SCRATCH = {
+    "srow": sb(16, "int32", 1), "sbc": sb(16, "int32"), "sf": sb(16, "float32"), "selv": sb(N, "float32"),
+    "snd": sb(SLOTS // 16, "int32"), "xo": sb(SLOTS // 16, "uint16"),
+    "ip": sb(32, "int32"), "ia": sb(32, "int32"), "ic": sb(32, "int32"), "base": sb(32, "float32"), "wo": sb(32 * N, "uint16"),
+    "pl": sb(32, "int32"), "ofl": sb(32, "int32"), "i1": sb(32, "float32"), "i2": sb(32, "float32"), "idx": sb(32, "uint16"),
+    "xt": sb(4 * TC, "bfloat16"), "xg": sb(4 * SLOTS, "bfloat16"), "xq": sb(SLOTS, CODE), "xs": sb(SLOTS, "uint8"),
+    "wt": sb(8 * NE, "bfloat16"), "wg": sb(4 * NE * N, "bfloat16"), "wq": sb(NE * N, CODE), "ws": sb(NE * N, "uint8"),
+    "xr": sb(SLOTS, CODE), "xrs": sb(SLOTS, "uint8"), "ew": sb(NE * N, CODE), "es": sb(NE * N, "uint8"),
+    "hx": sb(2 * CAPP, CODE), "hxs": sb(2 * CAPP, "uint8"), "hw": sb(2 * NE, CODE), "hws": sb(2 * NE, "uint8"),
+    "ps": ("psum", [128, 4096], "float32"), "res": sb(N * SLOTS, "float32"), "yt": sb(TC, "float32"),
+}
+SEMAPHORES = (["ldsel", "ldsnd", "ldx", "ldw", "ldi", "rep", "own", "yd", "iot", "ian", "bas", "selb", "sfd",
+               "selq", "seli", "selo", "ix1", "ix2", "ix3", "xin", "cpl", "gv", "gs", "sent", "hxc", "hxp", "hwc", "hwp"]
+              + [a + b for a in ("xo", "xg", "xq") for b in "01"] + [a + b for a in ("wo", "wg", "wq") for b in "QSPO"]
+              + [a + "%d" % k for a in ("we", "ma", "mb") for k in range(N)] + ["cp%d" % k for k in range(4)])
+
+
+def bits(es):
+    m = 0
+    for e in es:
+        m |= 1 << e
+    return m
+
+
+def plan(core, T, topo):
+    cores = list(T.cores)
+    chips = []
+    for c in cores:
+        if topo.chip(c) not in chips:
+            chips.append(topo.chip(c))
+    pair = [[r for r in range(N) if topo.chip(cores[r]) == h] for h in chips]
+    k = chips.index(topo.chip(core))
+    rest = [(k + i) % len(chips) for i in range(1, len(chips))]
+    same = [i for i in rest if topo.same_plane(chips[i], chips[k])]
+    cross = [i for i in rest if i not in same]
+    p = {"O": pair[k], "S": pair[same[0]], "P": pair[cross[0]], "Q": pair[cross[1]]}
+    mine = pair[k].index(T.rank_of(core))
+    away = [c for c in topo.cores_of(core) if c not in cores and topo.die(c) != topo.die(core)]
+    owners = [c for c in away if all(topo.may_write(c, cores[d]) for d in p["Q"])]
+    p["A"] = owners[mine]
+    p["B"] = [c for c in away if c not in owners][mine]
+    return p
+
+
+def tx(topo, c, mask, rs, src, dst):
+    rid, pid, _ = topo.addr(c)
+    if src.dtype == dt.float8_e4m3fn_x4:
+        src, dst = src.bitcast(dt.uint8), dst.bitcast(dt.uint8)
+    return RemoteDMATransfer(dst_ids=[DstId(rid=rid, pnc=pid)], dma_engine_mask=mask, remote_sem=rs, src=src, dst=dst)
+
+
+def helper_program(g, core, T, topo):
+    for r in range(N):
+        p = plan(T.cores[r], T, topo)
+        if core not in (p["A"], p["B"]):
+            continue
+        pair = p["Q"] if core == p["A"] else p["S"]
+        off = topo.engines(core, T.cores[pair[0]])
+        h = len(off) // 2
+        on = len(topo.engines(core, T.cores[r])) - len(off)
+        we = T.sem["we%d" % r]
+        jobs = [(T.sem.hxc, on // 2, T.hx, CAPP, T.xr, T.sem.xin), (T.sem.hxp, on // 2, T.hxs, CAPP, T.xrs, T.sem.xin)]
+        if core == p["A"]:
+            jobs += [(T.sem.hwc, on, T.hw, NE, T.ew, we), (T.sem.hwp, on, T.hws, NE, T.es, we)]
+        for sem, n, src, w, dst, rs in jobs:
+            g.wait_ge(sem, n)
+            g.remote_dma_fused([tx(topo, T.cores[d], bits(off[i * h:i * h + h]), rs, src[:, i * w:(i + 1) * w],
+                                   dst[:, r * w:(r + 1) * w]) for i, d in enumerate(pair)], local_sem=T.sem.sent)
+        g.wait_ge(T.sem.sent, 2 * h * len(jobs))
+
+
+def rank_program(g, core, T, topo):
+    r = T.rank_of(core)
+    if r is None:
+        return helper_program(g, core, T, topo)
+    V, S, PE, Y = g.vector, g.scalar, g.tensor, g.sync
+    sem, A = T.sem, AluOpType
+    COPY = ActivationFunctionType.Copy
+    cores = T.cores
+    p = plan(core, T, topo)
+    partner = [d for d in p["O"] if d != r][0]
+    order = p["Q"] + p["S"] + p["P"] + p["O"]
+    pos = {d: k for k, d in enumerate(order)}
+    off = topo.engines(core, cores[p["P"][0]])
+    on = [e for e in topo.engines(core, cores[partner]) if e not in off]
+    o4, n4 = len(off) // 2, len(on) // 2
+    offm, onm = [bits(off[:o4]), bits(off[o4:])], [bits(on[:n4]), bits(on[n4:])]
+
+    Y.dma_start(T.srow[0:1, :], T.sel[:]).then_inc(sem.ldsel, 16)
+    Y.dma_start(T.xt[0:64, :], T.x[0:64, :]).then_inc(sem.ldx, 16)
+    S.dma_start(T.xt[64:128, :], T.x[64:128, :]).then_inc(sem.ldx, 16)
+    for k in range(8):
+        q = Y if k % 2 else S
+        q.dma_start(T.snd[16 * k:16 * k + 16, :], T.send[:]).then_inc(sem.ldsnd, 16)
+    Y.dma_start(T.wt[:, 0:4 * NE], T.w[0:128, :]).then_inc(sem.ldw, 16)
+    S.dma_start(T.wt[:, 4 * NE:8 * NE], T.w[128:256, :]).then_inc(sem.ldw, 16)
+    Y.dma_start(T.pl[0:16, :], T.place[:]).then_inc(sem.ldi, 16)
+    Y.dma_start(T.ofl[0:16, :], T.of[:]).then_inc(sem.ldi, 16)
+
+    g.iota(T.ip[:], [[0, 32]], 0, 1).then_inc(sem.iot, 1)
+    g.iota(T.ic[:], [[16, 32]], 0, 0).then_inc(sem.iot, 1)
+    g.wait_ge(sem.ldsel, 16)
+    g.partition_broadcast(T.sbc[:], T.srow[0:1, :], 128).then_inc(sem.selb, 1)
+
+    V.wait_ge(sem.iot, 2)
+    V.tensor_scalar(T.ia[:], T.ip[:], 15, None, A.bitwise_and).then_inc(sem.ian, 1)
+    V.wait_ge(sem.ian, 1)
+    V.tensor_tensor(T.base[:], T.ia[:], T.ic[:], A.add).then_inc(sem.bas, 1)
+    V.wait_ge(sem.selb, 1)
+    V.tensor_scalar(T.sf[:], T.sbc[:], float(4 * NE), 0.0, A.mult, A.max).then_inc(sem.sfd, 1)
+
+    sent = 0
+    g.wait_ge(sem.sfd, 1)
+    two = [(d, off[2 * i:2 * i + 2], sem.seli) for i, d in enumerate(p["S"] + p["Q"])] + [(partner, on[:2], sem.selo)]
+    for call in ([(d, off[o4 * i:o4 * i + o4], sem.selq) for i, d in enumerate(p["P"])], two):
+        g.remote_dma_fused([tx(topo, cores[d], bits(es), s, T.sf[:, d:d + 1], T.selv[:, r:r + 1]) for d, es, s in call],
+                           local_sem=sem.sent)
+        sent += sum(len(es) for _, es, _ in call)
+    arrive = {"Q": (sem.selq, 2 * o4), "S": (sem.seli, 4 * 2), "O": (sem.selo, 2)}
+
+    V.wait_ge(sem.ldsnd, 128)
+    for k in range(4):
+        d = order[2 * k]
+        V.tensor_scalar(T.xo[:, 12 * k:12 * k + 12], T.snd[:, 6 * d:6 * d + 12], 4.0, 0.0, A.mult, A.max
+                        ).then_inc(sem["xo%d" % (k // 2)], 1)
+
+    def gather(q, a, b, t, s):
+        out, win = T.xg[:, 4 * a + t:4 * b:4], T.xt[:, t:4 * TC].indirect(T.xo[:, a // 16:b // 16])
+        (V.tensor_copy(out, win) if q is V else S.activation(out, win, COPY)).then_inc(s, 1)
+
+    for q in (V, S):
+        q.wait_ge(sem.ldx, 32)
+        for b in range(2):
+            a, e, s = HALF * b, HALF * (b + 1), sem["xg%d" % b]
+            c = e - (128 if b else 0)
+            q.wait_ge(sem["xo%d" % b], 2)
+            for (lo, hi, t) in (((a, e, 0), (a, c, 1)) if q is V else ((a, e, 2), (a, e, 3), (c, e, 1))):
+                if lo < hi:
+                    gather(q, lo, hi, t, s)
+            if q is V:
+                V.wait_ge(s, 4 + b)
+                V.quantize_mx(T.xq[:, a:e], T.xs[:, a:e], T.xg[:, 4 * a:4 * e]).then_inc(sem["xq%d" % b], 1)
+
+    a = CAPP * pos[r]
+    Y.wait_ge(sem.xq1, 1)
+    Y.dma_start(T.xr[:, CAPP * r:CAPP * (r + 1)].bitcast(dt.uint8), T.xq[:, a:a + CAPP].bitcast(dt.uint8)).then_inc(sem.own, 16)
+    Y.dma_start(T.xrs[:, CAPP * r:CAPP * (r + 1)], T.xs[:, a:a + CAPP]).then_inc(sem.own, 16)
+
+    def offs(c):
+        for d in p[c]:
+            col = T.sf[:, r:r + 1] if d == r else T.selv[:, d:d + 1]
+            V.tensor_scalar(T.wo[:, 32 * pos[d]:32 * pos[d] + 32], T.base[:], col, None, A.add).then_inc(sem["wo" + c], 1)
+
+    V.wait_ge(sem.bas, 1)
+    V.wait_ge(sem.ldw, 32)
+    S.wait_ge(sem.ldw, 32)
+    for k, (c, share) in enumerate((("Q", 512), ("S", 512), ("P", 384), ("O", 416))):
+        a, m, e = 1024 * k, 1024 * k + share, 1024 * (k + 1)
+        wo, wg = sem["wo" + c], sem["wg" + c]
+        if c in "QS":
+            V.wait_ge(*arrive[c])
+            offs(c)
+        S.wait_ge(wo, 2)
+        S.activation(T.wg[:, m:e], T.wt[:].indirect(T.wo[:, m // 16:e // 16]), COPY).then_inc(wg, 1)
+        V.wait_ge(wo, 2)
+        V.tensor_copy(T.wg[:, a:m], T.wt[:].indirect(T.wo[:, a // 16:m // 16])).then_inc(wg, 1)
+        if c == "S":
+            offs("P")
+            V.wait_ge(*arrive["O"])
+            offs("O")
+        V.wait_ge(wg, 2)
+        V.quantize_mx(T.wq[:, a // 4:e // 4], T.ws[:, a // 4:e // 4], T.wg[:, a:e]).then_inc(sem["wq" + c], 1)
+
+    V.wait_ge(sem.ldi, 32)
+    V.tensor_scalar(T.i1[0:16, :], T.ofl[0:16, :], float(SLOTS), None, A.mult).then_inc(sem.ix1, 1)
+    V.wait_ge(sem.ix1, 1)
+    V.tensor_tensor(T.i2[0:16, :], T.i1[0:16, :], T.pl[0:16, :], A.add).then_inc(sem.ix2, 1)
+    V.wait_ge(sem.ix2, 1)
+    V.tensor_copy(T.idx[0:16, :], T.i2[0:16, :]).then_inc(sem.ix3, 1)
+    Y.wait_ge(sem.ix3, 1)
+    for k in range(1, 8):
+        Y.dma_start(T.idx[16 * k:16 * k + 16, :], T.idx[0:16, :]).then_inc(sem.rep, 16)
+
+    def send(items):
+        for i in (0, 1):
+            g.remote_dma_fused([tx(topo, c, m, s[i], src[i][:, lo:hi], dst[i]) for c, m, s, src, lo, hi, dst in items],
+                               local_sem=sem.sent)
+        return 2 * sum(bin(m).count("1") for _, m, *_ in items)
+
+    def direct(d, m, w):
+        src, dst, s = (((T.xq, T.xs), (T.xr, T.xrs), sem.xin) if w == CAPP else ((T.wq, T.ws), (T.ew, T.es), sem["we%d" % r]))
+        return (cores[d], m, (s, s), src, w * pos[d], w * (pos[d] + 1), [t[:, w * r:w * (r + 1)] for t in dst])
+
+    def help_x(h, c, m):
+        return (p[h], m, (sem.hxc, sem.hxp), (T.xq, T.xs), CAPP * pos[p[c][0]], CAPP * (pos[p[c][0]] + 2), (T.hx[:], T.hxs[:]))
+
+    g.wait_ge(sem.xq0, 1)
+    sent += send([help_x("A", "Q", onm[0]), help_x("B", "S", onm[1])])
+    g.wait_ge(sem.xq1, 1)
+    sent += send([direct(d, offm[i], CAPP) for i, d in enumerate(p["P"])] + [direct(partner, bits(on), CAPP)])
+    g.wait_ge(sem.wqQ, 1)
+    sent += send([(p["A"], bits(on), (sem.hwc, sem.hwp), (T.wq, T.ws), 0, 2 * NE, (T.hw[:], T.hws[:]))])
+    for c in "SP":
+        g.wait_ge(sem["wq" + c], 1)
+        sent += send([direct(d, offm[i], NE) for i, d in enumerate(p[c])])
+    g.wait_ge(sem.wqO, 1)
+    sent += send([direct(partner, bits(on), NE)])
+    g.wait_ge(sem.sent, sent)
+
+    todo = [r] + p["S"] + [partner] + p["Q"] + p["P"]
+    PE.wait_ge(sem.own, 32)
+    PE.wait_ge(sem.xin, 6 * 2 * o4 + 2 * len(on))
+    for k, h in enumerate(todo):
+        if h == r:
+            PE.wait_ge(sem.wqO, 1)
+            st, ss = T.wq[:, NE * pos[r]:NE * (pos[r] + 1)], T.ws[:, NE * pos[r]:NE * (pos[r] + 1)]
+        else:
+            PE.wait_ge(sem["we%d" % h], 2 * (len(on) if h == partner else o4))
+            st, ss = T.ew[:, NE * h:NE * (h + 1)], T.es[:, NE * h:NE * (h + 1)]
+        if k >= 4:
+            PE.wait_ge(sem["cp%d" % (k - 4)], 2)
+        b = 1024 * (k % 4)
+        done = sem["cp%d" % k] if k < 4 else sem.cpl
+        for i, s in enumerate((sem["ma%d" % k], sem["mb%d" % k])):
+            x0, bank, out = HALF * i, T.ps[:, b + 512 * i:b + 512 * i + HALF], SLOTS * h + HALF * i
+            PE.matmul_mx(bank, st, ss, T.xr[:, x0:x0 + HALF], T.xrs[:, x0:x0 + HALF], True, True).then_inc(s, 1)
+            q = S if i else V
+            q.wait_ge(s, 1)
+            o = T.res[:, out:out + HALF]
+            (S.activation(o, bank, COPY) if i else V.tensor_copy(o, bank)).then_inc(done, 1)
+
+    h = TC // 2
+    for q in (V, S):
+        q.wait_ge(sem.rep, 112)
+        q.wait_ge(sem.ix3, 1)
+        q.wait_ge(sem.cpl, 8)
+    V.tensor_copy(T.yt[:, 0:h], T.res[:].indirect(T.idx[:, 0:16])).then_inc(sem.gv, 1)
+    S.activation(T.yt[:, h:TC], T.res[:].indirect(T.idx[:, 16:32]), COPY).then_inc(sem.gs, 1)
+    Y.wait_ge(sem.gv, 1)
+    Y.dma_start(T.y[:, 0:h], T.yt[:, 0:h]).then_inc(sem.yd, 16)
+    S.wait_ge(sem.gs, 1)
+    S.dma_start(T.y[:, h:TC], T.yt[:, h:TC]).then_inc(sem.yd, 16)
+    Y.wait_ge(sem.yd, 32)

@@ -1,4 +1,4 @@
-from concourse.bass import DstId, RemoteDMATransfer
+from concourse.bass import DstId, RemoteDMATransfer, IndirectOffsetOnAxis
 from concourse.mybir import dt, AluOpType, ActivationFunctionType
 
 N, TC, CAPP, NE = 8, 512, 96, 128
@@ -6,26 +6,45 @@ SLOTS = N * CAPP
 HALF = SLOTS // 2
 CODE = "float8_e4m3fn_x4"
 
+CFG = {
+    "make": ["xPS", "xQO", "wQ", "wS", "wP", "wO"],
+    "steps": [
+        ("xPS", [("P", "F0", "F1", "off"), ("S", "B", "C", "on")]),
+        ("xQO", [("Q0", "A", "A", "on0"), ("Q1", None, None, "off"), ("o", None, None, "on1")]),
+        ("wQ", [("Q0", "A", "A", "on"), ("Q1", None, None, "off")]),
+        ("wS", [("S0", "B", "B", "on"), ("S1", None, None, "off")]),
+        ("wP", [("P0", "A", "A", "on"), ("P1", None, None, "off")]),
+        ("wO", [("o", None, None, "on")]),
+    ],
+    "sel": [[("Q", None, "off"), ("O", None, "on0"), ("P", "A", "on1")], [("S", None, "off")]],
+    "vt": {"P": 384, "Q": 256},
+    "late": "", "early": False, "places": "last", "ownq": "wS",
+    "share": {"Q": 416, "S": 416, "P": 416, "O": 416},
+    "todo": "Q1 r S1 Q0 S0 P1 o P0",
+}
+
 
 def sb(n, t, p=128):
     return ("sbuf", [p, n], t)
 
 
 SCRATCH = {
-    "srow": sb(16, "int32", 1), "sbc": sb(16, "int32"), "sf": sb(16, "float32"), "selv": sb(N, "float32"),
+    "srow": sb(16, "int32", 1), "sbc": sb(16, "int32"), "sf": sb(16, "bfloat16"), "selv": sb(2 * N, "bfloat16"),
     "snd": sb(SLOTS // 16, "int32"), "xo": sb(SLOTS // 16, "uint16"),
     "ip": sb(32, "int32"), "ia": sb(32, "int32"), "ic": sb(32, "int32"), "base": sb(32, "float32"), "wo": sb(32 * N, "uint16"),
-    "pl": sb(32, "int32"), "ofl": sb(32, "int32"), "i1": sb(32, "float32"), "i2": sb(32, "float32"), "idx": sb(32, "uint16"),
+    "pl": sb(32, "int32"), "ofl": sb(32, "int32"), "i0": sb(32, "float32"), "i1": sb(32, "float32"), "i2": sb(32, "float32"),
+    "i3": sb(32, "float32"), "idx": sb(32, "uint16"), "pf": sb(1, "float32"), "row": sb(1, "int32"),
     "xt": sb(4 * TC, "bfloat16"), "xg": sb(4 * SLOTS, "bfloat16"), "xq": sb(SLOTS, CODE), "xs": sb(SLOTS, "uint8"),
     "wt": sb(8 * NE, "bfloat16"), "wg": sb(4 * NE * N, "bfloat16"), "wq": sb(NE * N, CODE), "ws": sb(NE * N, "uint8"),
-    "xr": sb(SLOTS, CODE), "xrs": sb(SLOTS, "uint8"), "ew": sb(NE * N, CODE), "es": sb(NE * N, "uint8"),
+    "xr": sb(SLOTS + CAPP, CODE), "xrs": sb(SLOTS + CAPP, "uint8"), "ew": sb(NE * N, CODE), "es": sb(NE * N, "uint8"),
     "hx": sb(2 * CAPP, CODE), "hxs": sb(2 * CAPP, "uint8"), "hw": sb(2 * NE, CODE), "hws": sb(2 * NE, "uint8"),
+    "hv": sb(2 * NE, CODE), "hvs": sb(2 * NE, "uint8"),
     "ps": ("psum", [128, 4096], "float32"), "res": sb(N * SLOTS, "float32"), "yt": sb(TC, "float32"),
 }
-SEMAPHORES = (["ldsel", "ldsnd", "ldx", "ldw", "ldi", "rep", "own", "yd", "iot", "ian", "bas", "selb", "sfd",
-               "selq", "seli", "selo", "ix1", "ix2", "ix3", "xin", "cpl", "gv", "gs", "sent", "hxc", "hxp", "hwc", "hwp"]
-              + [a + b for a in ("xo", "xg", "xq") for b in "01"] + [a + b for a in ("wo", "wg", "wq") for b in "QSPO"]
-              + [a + "%d" % k for a in ("we", "ma", "mb") for k in range(N)] + ["cp%d" % k for k in range(4)])
+SEMAPHORES = (["ldsel", "ldsnd", "ldx", "ldw", "ldi", "rep", "yd", "iot", "ian", "bas", "selb", "sfd", "xo",
+               "ix1", "ix2", "ix3", "ix4", "xin", "cpl", "gv", "gs", "sent", "hx0", "hx1", "hw0", "hw1", "hv0", "hv1", "hs", "row", "idr", "wr"]
+              + [a + b for a in ("sel", "xg", "x", "wo", "wg", "w") for b in "QSPO"]
+              + ["we%d" % k for k in range(N)] + ["mm%d" % k for k in range(2 * N)] + ["cp%d" % k for k in range(N)])
 
 
 def bits(es):
@@ -35,212 +54,296 @@ def bits(es):
     return m
 
 
-def plan(core, T, topo):
+def plan(r, T, topo):
     cores = list(T.cores)
+    core = cores[r]
     chips = []
     for c in cores:
         if topo.chip(c) not in chips:
             chips.append(topo.chip(c))
-    pair = [[r for r in range(N) if topo.chip(cores[r]) == h] for h in chips]
+    pair = [[d for d in range(N) if topo.chip(cores[d]) == h] for h in chips]
     k = chips.index(topo.chip(core))
     rest = [(k + i) % len(chips) for i in range(1, len(chips))]
     same = [i for i in rest if topo.same_plane(chips[i], chips[k])]
     cross = [i for i in rest if i not in same]
-    p = {"O": pair[k], "S": pair[same[0]], "P": pair[cross[0]], "Q": pair[cross[1]]}
-    mine = pair[k].index(T.rank_of(core))
-    away = [c for c in topo.cores_of(core) if c not in cores and topo.die(c) != topo.die(core)]
+    p = {"O": pair[k], "S": pair[same[0]], "Q": pair[cross[0]], "P": pair[cross[1]]}
+    mine = pair[k].index(r)
+    p["o"], p["r"] = [pair[k][1 - mine]], [r]
+    for c in "QSP":
+        p[c + "0"], p[c + "1"] = [p[c][mine]], [p[c][1 - mine]]
+    free = [c for c in topo.cores_of(core) if c not in cores]
+    away = [c for c in free if topo.die(c) != topo.die(core)]
     owners = [c for c in away if all(topo.may_write(c, cores[d]) for d in p["Q"])]
     p["A"] = owners[mine]
     p["B"] = [c for c in away if c not in owners][mine]
+    p["C"] = [c for c in free if c not in away][mine]
+    far = cores[p["P"][0]]
+    doors = [c for c in range(topo.CHIPS * topo.CORES_PER_CHIP) if topo.mates(topo.chip(c), topo.chip(far)) and topo.may_write(c, far)]
+    p["F0"], p["F1"] = doors[mine::2]
+    off = topo.engines(core, far)
+    on = [e for e in topo.engines(core, cores[p["o"][0]]) if e not in off]
+    for n, es in (("off", off), ("on", on)):
+        h = len(es) // 2
+        p[n], p[n + "0"], p[n + "1"] = es, es[:h], es[h:]
+        p[n + "2"], p[n + "3"] = es[h:h + h // 2], es[h + h // 2:]
+    p["all"] = off + on
+    p["start"] = (p["O"][0] + 2 * mine) % N
+    p["x0"] = CAPP * (1 - mine)
     return p
 
 
-def tx(topo, c, mask, rs, src, dst):
+def tx(topo, c, es, rs, src, dst):
     rid, pid, _ = topo.addr(c)
     if src.dtype == dt.float8_e4m3fn_x4:
         src, dst = src.bitcast(dt.uint8), dst.bitcast(dt.uint8)
-    return RemoteDMATransfer(dst_ids=[DstId(rid=rid, pnc=pid)], dma_engine_mask=mask, remote_sem=rs, src=src, dst=dst)
+    return RemoteDMATransfer(dst_ids=[DstId(rid=rid, pnc=pid)], dma_engine_mask=bits(es), remote_sem=rs, src=src, dst=dst)
 
 
-def helper_program(g, core, T, topo):
-    for r in range(N):
-        p = plan(T.cores[r], T, topo)
-        if core not in (p["A"], p["B"]):
-            continue
-        pair = p["Q"] if core == p["A"] else p["S"]
-        off = topo.engines(core, T.cores[pair[0]])
-        h = len(off) // 2
-        on = len(topo.engines(core, T.cores[r])) - len(off)
-        we = T.sem["we%d" % r]
-        jobs = [(T.sem.hxc, on // 2, T.hx, CAPP, T.xr, T.sem.xin), (T.sem.hxp, on // 2, T.hxs, CAPP, T.xrs, T.sem.xin)]
-        if core == p["A"]:
-            jobs += [(T.sem.hwc, on, T.hw, NE, T.ew, we), (T.sem.hwp, on, T.hws, NE, T.es, we)]
-        for sem, n, src, w, dst, rs in jobs:
-            g.wait_ge(sem, n)
-            g.remote_dma_fused([tx(topo, T.cores[d], bits(off[i * h:i * h + h]), rs, src[:, i * w:(i + 1) * w],
-                                   dst[:, r * w:(r + 1) * w]) for i, d in enumerate(pair)], local_sem=T.sem.sent)
-        g.wait_ge(T.sem.sent, 2 * h * len(jobs))
+def landing(T, plans, kind, s, d):
+    if kind == "x":
+        a = plans[d]["x0"] + CAPP * ((s - plans[d]["start"]) % N)
+        return T.xr[:, a:a + CAPP], T.xrs[:, a:a + CAPP], T.sem.xin
+    return T.ew[:, NE * s:NE * (s + 1)], T.es[:, NE * s:NE * (s + 1)], T.sem["we%d" % s]
+
+
+def last_hop(p, ranks, road, es):
+    return len(p[es]) if road is None else len(p["off"]) // len(p[ranks])
+
+
+def jobs():
+    out, seen = [], set()
+    for k, (ready, items) in enumerate(CFG["steps"]):
+        for i in (0, 1):
+            for ranks, *road, es in items:
+                h = "h" + ready[0]
+                if road[i] and (h, i, road[i]) in seen:
+                    h = "hv"
+                seen.add((h, i, road[i]))
+                out.append((k, ready, i, ranks, road[i], es, h))
+    return out
+
+
+def helper_program(g, core, T, topo, plans):
+    sent = 0
+    for r, p in enumerate(plans):
+        for c, road, es in [x for items in CFG["sel"] for x in items]:
+            if road and p[road] == core:
+                g.wait_ge(T.sem.hs, len(p[es]))
+                to, two = [s for s in range(N) if r in plans[s][c]], T.selv[:, 2 * r:2 * r + 2]
+                g.remote_dma_fused([tx(topo, T.cores[d], p["off%d" % i], T.sem["sel" + c], two, two)
+                                    for i, d in enumerate(to)], local_sem=T.sem.sent)
+                sent += len(p["off"])
+        for _, ready, i, ranks, road, es, h in jobs():
+            if road is None or p[road] != core:
+                continue
+            w, src = CAPP if ready[0] == "x" else NE, T[h + ("s" if i else "")]
+            n = last_hop(p, ranks, road, es)
+            g.wait_ge(T.sem["%s%d" % (h, i)], len(p[es]))
+            call = []
+            for j, d in enumerate(p[ranks]):
+                to = landing(T, plans, ready[0], r, d)
+                call.append(tx(topo, T.cores[d], p["off"][j * n:j * n + n], to[2], src[:, j * w:(j + 1) * w], to[i]))
+                sent += n
+            g.remote_dma_fused(call, local_sem=T.sem.sent)
+    if sent:
+        g.wait_ge(T.sem.sent, sent)
 
 
 def rank_program(g, core, T, topo):
+    plans = [plan(r, T, topo) for r in range(N)]
     r = T.rank_of(core)
     if r is None:
-        return helper_program(g, core, T, topo)
+        return helper_program(g, core, T, topo, plans)
     V, S, PE, Y = g.vector, g.scalar, g.tensor, g.sync
     sem, A = T.sem, AluOpType
     COPY = ActivationFunctionType.Copy
     cores = T.cores
-    p = plan(core, T, topo)
-    partner = [d for d in p["O"] if d != r][0]
-    order = p["Q"] + p["S"] + p["P"] + p["O"]
-    pos = {d: k for k, d in enumerate(order)}
-    off = topo.engines(core, cores[p["P"][0]])
-    on = [e for e in topo.engines(core, cores[partner]) if e not in off]
-    o4, n4 = len(off) // 2, len(on) // 2
-    offm, onm = [bits(off[:o4]), bits(off[o4:])], [bits(on[:n4]), bits(on[n4:])]
+    p = plans[r]
+    partner = p["o"][0]
+    make = CFG["make"]
+    idma = any(a == "own" for a, _ in CFG["steps"])
+    xb = [c for m in make if m[0] == "x" for c in m[1:]]
+    wb = [m[1] for m in make if m[0] == "w"]
+    pos = {d: k for k, d in enumerate(d for c in xb for d in (p[c] if c != "O" else p[c][::-1]))}
+    wpos = {d: k for k, d in enumerate(d for c in wb for d in p[c])}
 
     Y.dma_start(T.srow[0:1, :], T.sel[:]).then_inc(sem.ldsel, 16)
-    Y.dma_start(T.xt[0:64, :], T.x[0:64, :]).then_inc(sem.ldx, 16)
-    S.dma_start(T.xt[64:128, :], T.x[64:128, :]).then_inc(sem.ldx, 16)
     for k in range(8):
-        q = Y if k % 2 else S
-        q.dma_start(T.snd[16 * k:16 * k + 16, :], T.send[:]).then_inc(sem.ldsnd, 16)
-    Y.dma_start(T.wt[:, 0:4 * NE], T.w[0:128, :]).then_inc(sem.ldw, 16)
-    S.dma_start(T.wt[:, 4 * NE:8 * NE], T.w[128:256, :]).then_inc(sem.ldw, 16)
+        (Y if k % 2 else S).dma_start(T.snd[16 * k:16 * k + 16, :], T.send[:]).then_inc(sem.ldsnd, 16)
+    S.dma_start(T.xt[0:64, :], T.x[0:64, :]).then_inc(sem.ldx, 16)
+    Y.dma_start(T.xt[64:128, :], T.x[64:128, :]).then_inc(sem.ldx, 16)
+    S.dma_start(T.ofl[0:16, :], T.of[:]).then_inc(sem.ldi, 16)
     Y.dma_start(T.pl[0:16, :], T.place[:]).then_inc(sem.ldi, 16)
-    Y.dma_start(T.ofl[0:16, :], T.of[:]).then_inc(sem.ldi, 16)
+    S.dma_start(T.wt[:, 4 * NE:8 * NE], T.w[128:256, :]).then_inc(sem.ldw, 16)
+    Y.dma_start(T.wt[:, 0:4 * NE], T.w[0:128, :]).then_inc(sem.ldw, 16)
 
     g.iota(T.ip[:], [[0, 32]], 0, 1).then_inc(sem.iot, 1)
     g.iota(T.ic[:], [[16, 32]], 0, 0).then_inc(sem.iot, 1)
+    g.iota(T.pf[:], [[0, 1]], 0, 1, allow_small_or_imprecise_dtypes=True).then_inc(sem.iot, 1)
     g.wait_ge(sem.ldsel, 16)
     g.partition_broadcast(T.sbc[:], T.srow[0:1, :], 128).then_inc(sem.selb, 1)
 
-    V.wait_ge(sem.iot, 2)
+    V.wait_ge(sem.iot, 3)
     V.tensor_scalar(T.ia[:], T.ip[:], 15, None, A.bitwise_and).then_inc(sem.ian, 1)
     V.wait_ge(sem.ian, 1)
     V.tensor_tensor(T.base[:], T.ia[:], T.ic[:], A.add).then_inc(sem.bas, 1)
     V.wait_ge(sem.selb, 1)
     V.tensor_scalar(T.sf[:], T.sbc[:], float(4 * NE), 0.0, A.mult, A.max).then_inc(sem.sfd, 1)
-
-    sent = 0
-    g.wait_ge(sem.sfd, 1)
-    two = [(d, off[2 * i:2 * i + 2], sem.seli) for i, d in enumerate(p["S"] + p["Q"])] + [(partner, on[:2], sem.selo)]
-    for call in ([(d, off[o4 * i:o4 * i + o4], sem.selq) for i, d in enumerate(p["P"])], two):
-        g.remote_dma_fused([tx(topo, cores[d], bits(es), s, T.sf[:, d:d + 1], T.selv[:, r:r + 1]) for d, es, s in call],
-                           local_sem=sem.sent)
-        sent += sum(len(es) for _, es, _ in call)
-    arrive = {"Q": (sem.selq, 2 * o4), "S": (sem.seli, 4 * 2), "O": (sem.selo, 2)}
-
+    V.wait_ge(sem.sfd, 1)
+    if idma:
+        V.tensor_scalar(T.row[:], T.sf[:, r:r + 1], 0.25, T.pf[:], A.mult, A.add).then_inc(sem.row, 1)
     V.wait_ge(sem.ldsnd, 128)
-    for k in range(4):
-        d = order[2 * k]
-        V.tensor_scalar(T.xo[:, 12 * k:12 * k + 12], T.snd[:, 6 * d:6 * d + 12], 4.0, 0.0, A.mult, A.max
-                        ).then_inc(sem["xo%d" % (k // 2)], 1)
+    runs = [p[c] for c in xb if c != "O"] + [[d] for d in p["O"]]
+    for ds in runs:
+        a, d, n = 6 * pos[ds[0]], ds[0], 6 * len(ds)
+        V.tensor_scalar(T.xo[:, a:a + n], T.snd[:, 6 * d:6 * d + n], 4.0, 0.0, A.mult, A.max).then_inc(sem.xo, 1)
 
-    def gather(q, a, b, t, s):
-        out, win = T.xg[:, 4 * a + t:4 * b:4], T.xt[:, t:4 * TC].indirect(T.xo[:, a // 16:b // 16])
-        (V.tensor_copy(out, win) if q is V else S.activation(out, win, COPY)).then_inc(s, 1)
+    g.wait_ge(sem.sfd, 1)
+    to = {c: [s for s in range(N) if r in plans[s][c]] for c in wb[:3]}
+    sent = 0
+    for items in CFG["sel"]:
+        call = []
+        for c, road, es in items:
+            for i, d in enumerate([partner] if c == "O" else to[c][:1] if road else to[c]):
+                e, a = p[es] if c == "O" or road else p[es][i::2], plans[d]["O"][0]
+                call.append(tx(topo, p[road] if road else cores[d], e, sem.hs if road else sem["sel" + c], T.sf[:, a:a + 2],
+                               T.selv[:, 2 * r:2 * r + 2]))
+                sent += len(e)
+        g.remote_dma_fused(call, local_sem=sem.sent)
+    arrive = {c: len(p["off" if road else es]) for items in CFG["sel"] for c, road, es in items}
 
-    for q in (V, S):
-        q.wait_ge(sem.ldx, 32)
-        for b in range(2):
-            a, e, s = HALF * b, HALF * (b + 1), sem["xg%d" % b]
-            c = e - (128 if b else 0)
-            q.wait_ge(sem["xo%d" % b], 2)
-            for (lo, hi, t) in (((a, e, 0), (a, c, 1)) if q is V else ((a, e, 2), (a, e, 3), (c, e, 1))):
-                if lo < hi:
-                    gather(q, lo, hi, t, s)
-            if q is V:
-                V.wait_ge(s, 4 + b)
-                V.quantize_mx(T.xq[:, a:e], T.xs[:, a:e], T.xg[:, 4 * a:4 * e]).then_inc(sem["xq%d" % b], 1)
-
-    a = CAPP * pos[r]
-    Y.wait_ge(sem.xq1, 1)
-    Y.dma_start(T.xr[:, CAPP * r:CAPP * (r + 1)].bitcast(dt.uint8), T.xq[:, a:a + CAPP].bitcast(dt.uint8)).then_inc(sem.own, 16)
-    Y.dma_start(T.xrs[:, CAPP * r:CAPP * (r + 1)], T.xs[:, a:a + CAPP]).then_inc(sem.own, 16)
+    def picked(c):
+        return [partner] if c == "O" and idma else p[c]
 
     def offs(c):
-        for d in p[c]:
-            col = T.sf[:, r:r + 1] if d == r else T.selv[:, d:d + 1]
-            V.tensor_scalar(T.wo[:, 32 * pos[d]:32 * pos[d] + 32], T.base[:], col, None, A.add).then_inc(sem["wo" + c], 1)
+        V.wait_ge(sem["sel" + c], arrive[c])
+        for d in picked(c):
+            a = 2 * d + p["O"].index(r)
+            col = T.sf[:, r:r + 1] if d == r else T.selv[:, a:a + 1]
+            V.tensor_scalar(T.wo[:, 32 * wpos[d]:32 * wpos[d] + 32], T.base[:], col, None, A.add).then_inc(sem["wo" + c], 1)
 
+    def places():
+        first = float(CAPP * p["start"])
+        V.wait_ge(sem.ldi, 32)
+        V.tensor_scalar(T.i0[0:16, :], T.pl[0:16, :], first, float(SLOTS), A.is_lt, A.mult).then_inc(sem.ix1, 1)
+        V.tensor_scalar(T.i1[0:16, :], T.ofl[0:16, :], float(SLOTS), first, A.mult, A.subtract).then_inc(sem.ix1, 1)
+        V.wait_ge(sem.ix1, 2)
+        V.tensor_tensor(T.i2[0:16, :], T.i0[0:16, :], T.pl[0:16, :], A.add).then_inc(sem.ix2, 1)
+        V.wait_ge(sem.ix2, 1)
+        V.tensor_tensor(T.i3[0:16, :], T.i2[0:16, :], T.i1[0:16, :], A.add).then_inc(sem.ix4, 1)
+        V.wait_ge(sem.ix4, 1)
+        V.tensor_copy(T.idx[0:16, :], T.i3[0:16, :]).then_inc(sem.ix3, 1)
+        Y.wait_ge(sem.ix3, 1)
+        for k in range(1, 8):
+            Y.dma_start(T.idx[16 * k:16 * k + 16, :], T.idx[0:16, :]).then_inc(sem.rep, 16)
+
+    o0 = 0 if p["x0"] else SLOTS - CAPP
+    for q in (V, S):
+        q.wait_ge(sem.ldx, 32)
+        q.wait_ge(sem.xo, len(runs))
     V.wait_ge(sem.bas, 1)
-    V.wait_ge(sem.ldw, 32)
-    S.wait_ge(sem.ldw, 32)
-    for k, (c, share) in enumerate((("Q", 512), ("S", 512), ("P", 384), ("O", 416))):
-        a, m, e = 1024 * k, 1024 * k + share, 1024 * (k + 1)
-        wo, wg = sem["wo" + c], sem["wg" + c]
-        if c in "QS":
-            V.wait_ge(*arrive[c])
-            offs(c)
-        S.wait_ge(wo, 2)
-        S.activation(T.wg[:, m:e], T.wt[:].indirect(T.wo[:, m // 16:e // 16]), COPY).then_inc(wg, 1)
-        V.wait_ge(wo, 2)
-        V.tensor_copy(T.wg[:, a:m], T.wt[:].indirect(T.wo[:, a // 16:m // 16])).then_inc(wg, 1)
-        if c == "S":
-            offs("P")
-            V.wait_ge(*arrive["O"])
-            offs("O")
-        V.wait_ge(wg, 2)
-        V.quantize_mx(T.wq[:, a // 4:e // 4], T.ws[:, a // 4:e // 4], T.wg[:, a:e]).then_inc(sem["wq" + c], 1)
+    if CFG["places"] == "first":
+        places()
+    for m, nxt in zip(make, make[1:] + [None]):
+        kind, c = m[0], m[1]
+        s = sem[kind + "g" + c]
+        if kind == "x":
+            a = CAPP * min(pos[d] for d in p[c])
+            e = a + 2 * CAPP * len(m[1:])
+            cut = a + CFG["vt"][c]
+            parts = [(V, a, e, 0), (V, a, cut, 1), (S, a, e, 2), (S, a, e, 3), (S, cut, e, 1)]
+            parts = [x for x in parts if x[1] < x[2]]
+            for q, lo, hi, t in parts:
+                out, win = T.xg[:, 4 * lo + t:4 * hi:4], T.xt[:, t:4 * TC].indirect(T.xo[:, lo // 16:hi // 16])
+                (V.tensor_copy(out, win) if q is V else S.activation(out, win, COPY)).then_inc(s, 1)
+            if nxt[0] == "w" and CFG["early"]:
+                offs(nxt[1])
+            V.wait_ge(s, len(parts))
+            for c in m[1:]:
+                codes, plane, b = (T.xr, T.xrs, o0) if c == "O" else (T.xq, T.xs, a)
+                V.quantize_mx(codes[:, b:b + 2 * CAPP], plane[:, b:b + 2 * CAPP], T.xg[:, 4 * a:4 * (a + 2 * CAPP)]).then_inc(sem["x" + c], 1)
+                a += 2 * CAPP
+            if nxt[0] == "w" and not CFG["early"]:
+                offs(nxt[1])
+            continue
+        n = len(picked(c))
+        a = 4 * NE * wpos[picked(c)[0]]
+        mid, e = a + CFG["share"][c], a + 4 * NE * n
+        for q in (S, V):
+            q.wait_ge(sem.ldw, 32)
+            q.wait_ge(sem["wo" + c], n)
+        S.activation(T.wg[:, mid:e], T.wt[:].indirect(T.wo[:, mid // 16:e // 16]), COPY).then_inc(s, 1)
+        V.tensor_copy(T.wg[:, a:mid], T.wt[:].indirect(T.wo[:, a // 16:mid // 16])).then_inc(s, 1)
+        if nxt and nxt[1] not in CFG["late"]:
+            offs(nxt[1])
+        if m == CFG["places"]:
+            places()
+        V.wait_ge(s, 2)
+        V.quantize_mx(T.wq[:, a // 4:e // 4], T.ws[:, a // 4:e // 4], T.wg[:, a:e]).then_inc(sem[m], 1)
+        if nxt and nxt[1] in CFG["late"]:
+            offs(nxt[1])
+        if m == CFG["ownq"] and idma:
+            a = NE * wpos[r]
+            V.wait_ge(sem.idr, 16)
+            V.quantize_mx(T.wq[:, a:a + NE], T.ws[:, a:a + NE], T.wg[:, 4 * a:4 * (a + NE)]).then_inc(sem.wr, 1)
+    if CFG["places"] == "last":
+        places()
 
-    V.wait_ge(sem.ldi, 32)
-    V.tensor_scalar(T.i1[0:16, :], T.ofl[0:16, :], float(SLOTS), None, A.mult).then_inc(sem.ix1, 1)
-    V.wait_ge(sem.ix1, 1)
-    V.tensor_tensor(T.i2[0:16, :], T.i1[0:16, :], T.pl[0:16, :], A.add).then_inc(sem.ix2, 1)
-    V.wait_ge(sem.ix2, 1)
-    V.tensor_copy(T.idx[0:16, :], T.i2[0:16, :]).then_inc(sem.ix3, 1)
-    Y.wait_ge(sem.ix3, 1)
-    for k in range(1, 8):
-        Y.dma_start(T.idx[16 * k:16 * k + 16, :], T.idx[0:16, :]).then_inc(sem.rep, 16)
-
-    def send(items):
+    js = jobs()
+    for k, (ready, _) in enumerate(CFG["steps"]):
+        if ready == "own":
+            a = 4 * NE * wpos[r]
+            g.wait_ge(sem.row, 1)
+            g.indirect_dma_start(T.wg[:, a:a + 4 * NE], None, T.w[:], IndirectOffsetOnAxis(ap=T.row[:], axis=0),
+                                 bounds_check=2 * NE - 1).then_inc(sem.idr, 16)
+            continue
+        for c in ready[1:]:
+            g.wait_ge(sem[ready[0] + c], 1)
+        kind = ready[0]
         for i in (0, 1):
-            g.remote_dma_fused([tx(topo, c, m, s[i], src[i][:, lo:hi], dst[i]) for c, m, s, src, lo, hi, dst in items],
-                               local_sem=sem.sent)
-        return 2 * sum(bin(m).count("1") for _, m, *_ in items)
-
-    def direct(d, m, w):
-        src, dst, s = (((T.xq, T.xs), (T.xr, T.xrs), sem.xin) if w == CAPP else ((T.wq, T.ws), (T.ew, T.es), sem["we%d" % r]))
-        return (cores[d], m, (s, s), src, w * pos[d], w * (pos[d] + 1), [t[:, w * r:w * (r + 1)] for t in dst])
-
-    def help_x(h, c, m):
-        return (p[h], m, (sem.hxc, sem.hxp), (T.xq, T.xs), CAPP * pos[p[c][0]], CAPP * (pos[p[c][0]] + 2), (T.hx[:], T.hxs[:]))
-
-    g.wait_ge(sem.xq0, 1)
-    sent += send([help_x("A", "Q", onm[0]), help_x("B", "S", onm[1])])
-    g.wait_ge(sem.xq1, 1)
-    sent += send([direct(d, offm[i], CAPP) for i, d in enumerate(p["P"])] + [direct(partner, bits(on), CAPP)])
-    g.wait_ge(sem.wqQ, 1)
-    sent += send([(p["A"], bits(on), (sem.hwc, sem.hwp), (T.wq, T.ws), 0, 2 * NE, (T.hw[:], T.hws[:]))])
-    for c in "SP":
-        g.wait_ge(sem["wq" + c], 1)
-        sent += send([direct(d, offm[i], NE) for i, d in enumerate(p[c])])
-    g.wait_ge(sem.wqO, 1)
-    sent += send([direct(partner, bits(on), NE)])
+            call = []
+            for _, _, _, ranks, road, es, h in [j for j in js if j[0] == k and j[2] == i]:
+                ds = p[ranks]
+                if kind == "x" and ranks == "o":
+                    src, a, w = (T.xr, T.xrs)[i], (0 if p["x0"] else SLOTS), CAPP
+                elif kind == "x":
+                    src, a, w = (T.xq, T.xs)[i], CAPP * pos[ds[0]], CAPP * len(ds)
+                else:
+                    src, a, w = (T.wq, T.ws)[i], NE * wpos[ds[0]], NE * len(ds)
+                if road is None:
+                    at = landing(T, plans, kind, r, ds[0])
+                    call.append(tx(topo, cores[ds[0]], p[es], at[2], src[:, a:a + w], at[i]))
+                else:
+                    call.append(tx(topo, p[road], p[es], sem["%s%d" % (h, i)], src[:, a:a + w], T[h + ("s" if i else "")][:, 0:w]))
+                sent += len(p[es])
+            g.remote_dma_fused(call, local_sem=sem.sent)
     g.wait_ge(sem.sent, sent)
 
-    todo = [r] + p["S"] + [partner] + p["Q"] + p["P"]
-    PE.wait_ge(sem.own, 32)
-    PE.wait_ge(sem.xin, 6 * 2 * o4 + 2 * len(on))
-    for k, h in enumerate(todo):
+    come = {}
+    for s in range(N):
+        for _, ready, i, ranks, road, es, _ in js:
+            if r in plans[s][ranks]:
+                key = "xin" if ready[0] == "x" else "we%d" % s
+                come[key] = come.get(key, 0) + last_hop(plans[s], ranks, road, es)
+    PE.wait_ge(sem.xin, come["xin"])
+    PE.wait_ge(sem.xO, 1)
+    for j, c in enumerate(CFG["todo"].split()):
+        h = [s for s in range(N) if r in plans[s][c]][0]
         if h == r:
-            PE.wait_ge(sem.wqO, 1)
-            st, ss = T.wq[:, NE * pos[r]:NE * (pos[r] + 1)], T.ws[:, NE * pos[r]:NE * (pos[r] + 1)]
+            PE.wait_ge(sem.wr if idma else sem.wO, 1)
+            st, ss = T.wq[:, NE * wpos[r]:NE * (wpos[r] + 1)], T.ws[:, NE * wpos[r]:NE * (wpos[r] + 1)]
         else:
-            PE.wait_ge(sem["we%d" % h], 2 * (len(on) if h == partner else o4))
+            PE.wait_ge(sem["we%d" % h], come["we%d" % h])
             st, ss = T.ew[:, NE * h:NE * (h + 1)], T.es[:, NE * h:NE * (h + 1)]
-        if k >= 4:
-            PE.wait_ge(sem["cp%d" % (k - 4)], 2)
-        b = 1024 * (k % 4)
-        done = sem["cp%d" % k] if k < 4 else sem.cpl
-        for i, s in enumerate((sem["ma%d" % k], sem["mb%d" % k])):
-            x0, bank, out = HALF * i, T.ps[:, b + 512 * i:b + 512 * i + HALF], SLOTS * h + HALF * i
-            PE.matmul_mx(bank, st, ss, T.xr[:, x0:x0 + HALF], T.xrs[:, x0:x0 + HALF], True, True).then_inc(s, 1)
-            q = S if i else V
-            q.wait_ge(s, 1)
-            o = T.res[:, out:out + HALF]
-            (S.activation(o, bank, COPY) if i else V.tensor_copy(o, bank)).then_inc(done, 1)
+        for i in (0, 1):
+            k = 2 * j + i
+            if k >= 8:
+                PE.wait_ge(sem["cp%d" % (k - 8)], 1)
+            x0, bank, out = p["x0"] + HALF * i, T.ps[:, 512 * (k % 8):512 * (k % 8) + HALF], SLOTS * h + HALF * i
+            PE.matmul_mx(bank, st, ss, T.xr[:, x0:x0 + HALF], T.xrs[:, x0:x0 + HALF], True, True).then_inc(sem["mm%d" % k], 1)
+            q, o = (S if i else V), T.res[:, out:out + HALF]
+            q.wait_ge(sem["mm%d" % k], 1)
+            (S.activation(o, bank, COPY) if i else V.tensor_copy(o, bank)).then_inc(sem["cp%d" % k] if k < 8 else sem.cpl, 1)
 
     h = TC // 2
     for q in (V, S):
@@ -250,7 +353,6 @@ def rank_program(g, core, T, topo):
     V.tensor_copy(T.yt[:, 0:h], T.res[:].indirect(T.idx[:, 0:16])).then_inc(sem.gv, 1)
     S.activation(T.yt[:, h:TC], T.res[:].indirect(T.idx[:, 16:32]), COPY).then_inc(sem.gs, 1)
     Y.wait_ge(sem.gv, 1)
-    Y.dma_start(T.y[:, 0:h], T.yt[:, 0:h]).then_inc(sem.yd, 16)
-    S.wait_ge(sem.gs, 1)
-    S.dma_start(T.y[:, h:TC], T.yt[:, h:TC]).then_inc(sem.yd, 16)
-    Y.wait_ge(sem.yd, 32)
+    Y.wait_ge(sem.gs, 1)
+    Y.dma_start(T.y[:], T.yt[:]).then_inc(sem.yd, 16)
+    Y.wait_ge(sem.yd, 16)

@@ -1,26 +1,29 @@
-from concourse.bass import DstId, RemoteDMATransfer, IndirectOffsetOnAxis
+from concourse.bass import DstId, RemoteDMATransfer
 from concourse.mybir import dt, AluOpType, ActivationFunctionType
 
 N, TC, CAPP, NE = 8, 512, 96, 128
 SLOTS = N * CAPP
-HALF = SLOTS // 2
+BANK = 512
 CODE = "float8_e4m3fn_x4"
+NAMES = ["Q0", "Q1", "S0", "S1", "P0", "P1", "o", "r"]
 
 CFG = {
-    "make": ["xPS", "xQO", "wQ", "wS", "wP", "wO"],
+    "make": [("x", "P S", 384), ("x", "Q1 Q0 o r", 256), ("w", "Q0 Q1", 512), ("w", "S0 P0", 448), ("w", "S1 P1", 448),
+             ("w", "o r", 320)],
+    "pre": 256, "places": "last", "flip": 0, "late": [2], "dsel": 0, "ownlate": 2, "ahead": [5], "out": [128, 128], "head": 32,
+    "stagger": range(N),
     "steps": [
-        ("xPS", [("P", "F0", "F1", "off"), ("S", "B", "C", "on")]),
-        ("xQO", [("Q0", "A", "A", "on0"), ("Q1", None, None, "off"), ("o", None, None, "on1")]),
-        ("wQ", [("Q0", "A", "A", "on"), ("Q1", None, None, "off")]),
-        ("wS", [("S0", "B", "B", "on"), ("S1", None, None, "off")]),
-        ("wP", [("P0", "A", "A", "on"), ("P1", None, None, "off")]),
-        ("wO", [("o", None, None, "on")]),
+        (0, [("P", "F0", "F1", "off"), ("S", "B", "C", "on")]),
+        (1, [("Q0+o", "A", "A", "on")]),
+        (1, [("Q1", None, None, "off")]),
+        (2, [("Q0", "A", "A", "on"), ("Q1", None, None, "off")]),
+        (3, [("S0", "B", "B", "on"), ("P0", None, None, "off")]),
+        (4, [("S1", "B", "B", "on"), ("P1", None, None, "off")]),
+        (5, [("o", None, None, "on")]),
     ],
-    "sel": [[("Q", None, "off"), ("O", None, "on0"), ("P", "A", "on1")], [("S", None, "off")]],
-    "vt": {"P": 384, "Q": 256},
-    "late": "", "early": False, "places": "last", "ownq": "wS",
-    "share": {"Q": 416, "S": 416, "P": 416, "O": 416},
-    "todo": "Q1 r S1 Q0 S0 P1 o P0",
+    "sel": [[("Q0", None, "off0"), ("Q1", None, "off1"), ("S1", "B", "on0"), ("P1", "A", "on1")],
+            [("S0", None, "off0"), ("P0", None, "off1"), ("o", None, "on0")]],
+    "todo": "Q1a Q1b ra rb P0a P0b Q0a Q0b S0a S0b oa ob P1a P1b S1a S1b",
 }
 
 
@@ -30,21 +33,20 @@ def sb(n, t, p=128):
 
 SCRATCH = {
     "srow": sb(16, "int32", 1), "sbc": sb(16, "int32"), "sf": sb(16, "bfloat16"), "selv": sb(2 * N, "bfloat16"),
+    "sd": ("dram", [128, 2], "int32"), "land": ("dram", [N, 128, 2], "int32"), "wrow": sb(16, "int32", 1), "wbc": sb(16, "int32"),
     "snd": sb(SLOTS // 16, "int32"), "xo": sb(SLOTS // 16, "uint16"),
     "ip": sb(32, "int32"), "ia": sb(32, "int32"), "ic": sb(32, "int32"), "base": sb(32, "float32"), "wo": sb(32 * N, "uint16"),
-    "pl": sb(32, "int32"), "ofl": sb(32, "int32"), "i0": sb(32, "float32"), "i1": sb(32, "float32"), "i2": sb(32, "float32"),
-    "i3": sb(32, "float32"), "idx": sb(32, "uint16"), "pf": sb(1, "float32"), "row": sb(1, "int32"),
+    "pl": sb(32, "int32"), "ofl": sb(32, "int32"), "ix": sb(32 * 4, "float32"), "idx": sb(32, "uint16"),
     "xt": sb(4 * TC, "bfloat16"), "xg": sb(4 * SLOTS, "bfloat16"), "xq": sb(SLOTS, CODE), "xs": sb(SLOTS, "uint8"),
     "wt": sb(8 * NE, "bfloat16"), "wg": sb(4 * NE * N, "bfloat16"), "wq": sb(NE * N, CODE), "ws": sb(NE * N, "uint8"),
     "xr": sb(SLOTS + CAPP, CODE), "xrs": sb(SLOTS + CAPP, "uint8"), "ew": sb(NE * N, CODE), "es": sb(NE * N, "uint8"),
-    "hx": sb(2 * CAPP, CODE), "hxs": sb(2 * CAPP, "uint8"), "hw": sb(2 * NE, CODE), "hws": sb(2 * NE, "uint8"),
-    "hv": sb(2 * NE, CODE), "hvs": sb(2 * NE, "uint8"),
+    **{"h%d" % k: sb(3 * NE, CODE) for k in range(N + 1)}, **{"hs%d" % k: sb(3 * NE, "uint8") for k in range(N + 1)},
     "ps": ("psum", [128, 4096], "float32"), "res": sb(N * SLOTS, "float32"), "yt": sb(TC, "float32"),
 }
-SEMAPHORES = (["ldsel", "ldsnd", "ldx", "ldw", "ldi", "rep", "yd", "iot", "ian", "bas", "selb", "sfd", "xo",
-               "ix1", "ix2", "ix3", "ix4", "xin", "cpl", "gv", "gs", "sent", "hx0", "hx1", "hw0", "hw1", "hv0", "hv1", "hs", "row", "idr", "wr"]
-              + [a + b for a in ("sel", "xg", "x", "wo", "wg", "w") for b in "QSPO"]
-              + ["we%d" % k for k in range(N)] + ["mm%d" % k for k in range(2 * N)] + ["cp%d" % k for k in range(N)])
+SEMAPHORES = (["ldsel", "ldsnd", "ldx", "ldw", "ldi", "rep", "yd", "iot", "ian", "bas", "selb", "sfd", "xo", "own", "pre", "xown", "ldsd", "ldown", "ldwish", "wbc", "wf",
+               "idx", "xfar", "xnear", "cpl", "gv", "gs", "sent", "hsel", "ix0", "ix1", "ix2"] + ["sel" + n for n in NAMES]
+              + [a + "%d" % k for a in ("we", "cp", "wo", "got", "made", "hc", "hp") for k in range(N + 1)] + ["mm%d" % k for k in range(2 * N)])
+WIDTH = {"x": CAPP, "w": NE}
 
 
 def bits(es):
@@ -66,7 +68,7 @@ def plan(r, T, topo):
     rest = [(k + i) % len(chips) for i in range(1, len(chips))]
     same = [i for i in rest if topo.same_plane(chips[i], chips[k])]
     cross = [i for i in rest if i not in same]
-    p = {"O": pair[k], "S": pair[same[0]], "Q": pair[cross[0]], "P": pair[cross[1]]}
+    p = {"O": pair[k][::-1], "S": pair[same[0]], "P": pair[cross[0]], "Q": pair[cross[1]]}
     mine = pair[k].index(r)
     p["o"], p["r"] = [pair[k][1 - mine]], [r]
     for c in "QSP":
@@ -80,6 +82,9 @@ def plan(r, T, topo):
     far = cores[p["P"][0]]
     doors = [c for c in range(topo.CHIPS * topo.CORES_PER_CHIP) if topo.mates(topo.chip(c), topo.chip(far)) and topo.may_write(c, far)]
     p["F0"], p["F1"] = doors[mine::2]
+    far2 = cores[p["Q"][0]]
+    doors = [c for c in range(topo.CHIPS * topo.CORES_PER_CHIP) if topo.mates(topo.chip(c), topo.chip(far2)) and topo.may_write(c, far2)]
+    p["G0"], p["G1"] = doors[mine::2]
     off = topo.engines(core, far)
     on = [e for e in topo.engines(core, cores[p["o"][0]]) if e not in off]
     for n, es in (("off", off), ("on", on)):
@@ -87,9 +92,18 @@ def plan(r, T, topo):
         p[n], p[n + "0"], p[n + "1"] = es, es[:h], es[h:]
         p[n + "2"], p[n + "3"] = es[h:h + h // 2], es[h + h // 2:]
     p["all"] = off + on
-    p["start"] = (p["O"][0] + 2 * mine) % N
-    p["x0"] = CAPP * (1 - mine)
+    p["a0"], p["a1"] = off[0:2], off[2:4]
+    p["first"] = mine == 0
+    p["start"] = r
+    p["x0"] = NE - CAPP
+    for _, items in CFG["steps"]:
+        for ns, *_ in items:
+            p[ns] = [d for n in ns.split("+") for d in p[n]]
     return p
+
+
+def knows(plans, r, name):
+    return [s for s in range(N) if r in plans[s][name]][0]
 
 
 def tx(topo, c, es, rs, src, dst):
@@ -102,48 +116,49 @@ def tx(topo, c, es, rs, src, dst):
 def landing(T, plans, kind, s, d):
     if kind == "x":
         a = plans[d]["x0"] + CAPP * ((s - plans[d]["start"]) % N)
-        return T.xr[:, a:a + CAPP], T.xrs[:, a:a + CAPP], T.sem.xin
-    return T.ew[:, NE * s:NE * (s + 1)], T.es[:, NE * s:NE * (s + 1)], T.sem["we%d" % s]
+        return T.xr[:, a:a + CAPP], T.xrs[:, a:a + CAPP], "xnear" if s in plans[d]["O"] else "xfar"
+    return T.ew[:, NE * s:NE * (s + 1)], T.es[:, NE * s:NE * (s + 1)], "we%d" % s
 
 
-def last_hop(p, ranks, road, es):
-    return len(p[es]) if road is None else len(p["off"]) // len(p[ranks])
+def last_hop(p, ranks, road, es, d):
+    if road is None:
+        return p[es]
+    if d in p["o"]:
+        return p["on"]
+    far = [x for x in p[ranks] if x not in p["o"]]
+    n = len(p["off"]) // len(far)
+    return p["off"][n * far.index(d):n * far.index(d) + n]
 
 
-def jobs():
-    out, seen = [], set()
-    for k, (ready, items) in enumerate(CFG["steps"]):
-        for i in (0, 1):
-            for ranks, *road, es in items:
-                h = "h" + ready[0]
-                if road[i] and (h, i, road[i]) in seen:
-                    h = "hv"
-                seen.add((h, i, road[i]))
-                out.append((k, ready, i, ranks, road[i], es, h))
-    return out
+def jobs(p):
+    return [(k, m, CFG["make"][m][0], i, ranks, road[i], es) for k, (m, items) in enumerate(CFG["steps"])
+            for i in turn(p, k) for ranks, *road, es in items]
+
+
+def turn(p, k):
+    return (0, 1) if p["first"] or k not in CFG["stagger"] else (1, 0)
 
 
 def helper_program(g, core, T, topo, plans):
     sent = 0
     for r, p in enumerate(plans):
-        for c, road, es in [x for items in CFG["sel"] for x in items]:
-            if road and p[road] == core:
-                g.wait_ge(T.sem.hs, len(p[es]))
-                to, two = [s for s in range(N) if r in plans[s][c]], T.selv[:, 2 * r:2 * r + 2]
-                g.remote_dma_fused([tx(topo, T.cores[d], p["off%d" % i], T.sem["sel" + c], two, two)
-                                    for i, d in enumerate(to)], local_sem=T.sem.sent)
-                sent += len(p["off"])
-        for _, ready, i, ranks, road, es, h in jobs():
+        for c, road, es in [x for items in CFG["sel"] for x in items if x[1] and p[x[1]] == core]:
+            g.wait_ge(T.sem.hsel, len(p[es]))
+            ns = [c + "0", c + "1"] if c in "PQS" else [c]
+            n, two = len(p["off"]) // len(ns), T.selv[:, 2 * r:2 * r + 2]
+            g.remote_dma_fused([tx(topo, T.cores[knows(plans, r, x)], p["off"][j * n:j * n + n], T.sem["sel" + x], two, two)
+                                for j, x in enumerate(ns)], local_sem=T.sem.sent)
+            sent += len(p["off"])
+        for k, _, kind, i, ranks, road, es in jobs(p):
             if road is None or p[road] != core:
                 continue
-            w, src = CAPP if ready[0] == "x" else NE, T[h + ("s" if i else "")]
-            n = last_hop(p, ranks, road, es)
-            g.wait_ge(T.sem["%s%d" % (h, i)], len(p[es]))
+            w, src = WIDTH[kind], T[("h%d", "hs%d")[i] % k]
+            g.wait_ge(T.sem[("hc%d", "hp%d")[i] % k], len(p[es]))
             call = []
             for j, d in enumerate(p[ranks]):
-                to = landing(T, plans, ready[0], r, d)
-                call.append(tx(topo, T.cores[d], p["off"][j * n:j * n + n], to[2], src[:, j * w:(j + 1) * w], to[i]))
-                sent += n
+                to, by = landing(T, plans, kind, r, d), last_hop(p, ranks, road, es, d)
+                call.append(tx(topo, T.cores[d], by, T.sem[to[2]], src[:, j * w:(j + 1) * w], to[i]))
+                sent += len(by)
             g.remote_dma_fused(call, local_sem=T.sem.sent)
     if sent:
         g.wait_ge(T.sem.sent, sent)
@@ -159,200 +174,263 @@ def rank_program(g, core, T, topo):
     COPY = ActivationFunctionType.Copy
     cores = T.cores
     p = plans[r]
-    partner = p["o"][0]
-    make = CFG["make"]
-    idma = any(a == "own" for a, _ in CFG["steps"])
-    xb = [c for m in make if m[0] == "x" for c in m[1:]]
-    wb = [m[1] for m in make if m[0] == "w"]
-    pos = {d: k for k, d in enumerate(d for c in xb for d in (p[c] if c != "O" else p[c][::-1]))}
-    wpos = {d: k for k, d in enumerate(d for c in wb for d in p[c])}
+    make = [(kind, ns.split(), share) for kind, ns, share in CFG["make"]]
+    pos = {kind: {d: k for k, d in enumerate(d for a, ns, _ in make if a == kind for n in ns for d in p[n])} for kind in "xw"}
+    name = {p[n][0]: n for n in NAMES}
+    pre = CFG["pre"]
+    got = []
 
-    Y.dma_start(T.srow[0:1, :], T.sel[:]).then_inc(sem.ldsel, 16)
+    def lists():
+        S.dma_start(T.ofl[0:16, :], T.of[:]).then_inc(sem.ldi, 16)
+        Y.dma_start(T.pl[0:16, :], T.place[:]).then_inc(sem.ldi, 16)
+
+    if CFG["dsel"]:
+        Y.dma_start(T.sd[0:8, :], T.sel[:]).then_inc(sem.ldsd, 16)
+    (S if CFG["dsel"] else Y).dma_start(T.srow[0:1, :], T.sel[:]).then_inc(sem.ldsel, 16)
+    cut = CFG["head"] or 64
+    if CFG["head"]:
+        S.dma_start(T.xt[0:cut, :], T.x[0:cut, :]).then_inc(sem.ldx, 16)
     for k in range(8):
         (Y if k % 2 else S).dma_start(T.snd[16 * k:16 * k + 16, :], T.send[:]).then_inc(sem.ldsnd, 16)
-    S.dma_start(T.xt[0:64, :], T.x[0:64, :]).then_inc(sem.ldx, 16)
-    Y.dma_start(T.xt[64:128, :], T.x[64:128, :]).then_inc(sem.ldx, 16)
-    S.dma_start(T.ofl[0:16, :], T.of[:]).then_inc(sem.ldi, 16)
-    Y.dma_start(T.pl[0:16, :], T.place[:]).then_inc(sem.ldi, 16)
-    S.dma_start(T.wt[:, 4 * NE:8 * NE], T.w[128:256, :]).then_inc(sem.ldw, 16)
+    if CFG["places"] == "first":
+        lists()
+    if not CFG["head"]:
+        S.dma_start(T.xt[0:cut, :], T.x[0:cut, :]).then_inc(sem.ldx, 16)
+    Y.dma_start(T.xt[cut:128, :], T.x[cut:128, :]).then_inc(sem.ldx, 16)
+    if CFG["places"] != "first":
+        lists()
+    Y.dma_start(T.wt[:, 4 * NE:8 * NE], T.w[128:256, :]).then_inc(sem.ldw, 16)
     Y.dma_start(T.wt[:, 0:4 * NE], T.w[0:128, :]).then_inc(sem.ldw, 16)
+    if CFG["dsel"]:
+        S.dma_start(T.land[r, 0:8, :], T.sel[:]).then_inc(sem.ldown, 16)
 
     g.iota(T.ip[:], [[0, 32]], 0, 1).then_inc(sem.iot, 1)
     g.iota(T.ic[:], [[16, 32]], 0, 0).then_inc(sem.iot, 1)
-    g.iota(T.pf[:], [[0, 1]], 0, 1, allow_small_or_imprecise_dtypes=True).then_inc(sem.iot, 1)
-    g.wait_ge(sem.ldsel, 16)
-    g.partition_broadcast(T.sbc[:], T.srow[0:1, :], 128).then_inc(sem.selb, 1)
+    if CFG["dsel"]:
+        g.wait_ge(sem.ldsd, 16)
+    else:
+        g.wait_ge(sem.ldsel, 16)
+        g.partition_broadcast(T.sbc[:], T.srow[0:1, :], 128).then_inc(sem.selb, 1)
 
-    V.wait_ge(sem.iot, 3)
+    def offs(ns, s):
+        for d in [d for n in ns for d in p[n]]:
+            if d != r and CFG["dsel"]:
+                if not got:
+                    V.wait_ge(sem.wbc, 1)
+                    V.tensor_scalar(T.selv[:], T.wbc[:], float(4 * NE), 0.0, A.mult, A.max).then_inc(sem.wf, 1)
+                    V.wait_ge(sem.wf, 1)
+                    got.append(1)
+            elif d != r:
+                V.wait_ge(sem["sel" + name[d]], arrive[name[d]])
+            b = 2 * d + r - min(p["O"])
+            a, col = 32 * pos["w"][d], T.sf[:, r:r + 1] if d == r else T.selv[:, b:b + 1]
+            V.tensor_scalar(T.wo[:, a:a + 32], T.base[:], col, None, A.add).then_inc(s, 1)
+
+    V.wait_ge(sem.iot, 2)
     V.tensor_scalar(T.ia[:], T.ip[:], 15, None, A.bitwise_and).then_inc(sem.ian, 1)
     V.wait_ge(sem.ian, 1)
     V.tensor_tensor(T.base[:], T.ia[:], T.ic[:], A.add).then_inc(sem.bas, 1)
     V.wait_ge(sem.selb, 1)
     V.tensor_scalar(T.sf[:], T.sbc[:], float(4 * NE), 0.0, A.mult, A.max).then_inc(sem.sfd, 1)
     V.wait_ge(sem.sfd, 1)
-    if idma:
-        V.tensor_scalar(T.row[:], T.sf[:, r:r + 1], 0.25, T.pf[:], A.mult, A.add).then_inc(sem.row, 1)
+    V.wait_ge(sem.bas, 1)
+    offs(["r"], sem.own)
     V.wait_ge(sem.ldsnd, 128)
-    runs = [p[c] for c in xb if c != "O"] + [[d] for d in p["O"]]
+    runs = []
+    for d in pos["x"]:
+        if runs and runs[-1][-1] + 1 == d:
+            runs[-1].append(d)
+        else:
+            runs.append([d])
     for ds in runs:
-        a, d, n = 6 * pos[ds[0]], ds[0], 6 * len(ds)
+        a, d, n = 6 * pos["x"][ds[0]], ds[0], 6 * len(ds)
         V.tensor_scalar(T.xo[:, a:a + n], T.snd[:, 6 * d:6 * d + n], 4.0, 0.0, A.mult, A.max).then_inc(sem.xo, 1)
 
-    g.wait_ge(sem.sfd, 1)
-    to = {c: [s for s in range(N) if r in plans[s][c]] for c in wb[:3]}
     sent = 0
+    if CFG["dsel"]:
+        es = p["off"][:6] + p["on"][:1]
+        others = [knows(plans, r, n) for n in NAMES[:7]]
+        g.remote_dma_fused([tx(topo, cores[d], [e], sem.hsel, T.sd[:], T.land[r]) for d, e in zip(others, es)], local_sem=sem.sent)
+        sent += 7
+        g.wait_ge(sem.ldsel, 16)
+        g.partition_broadcast(T.sbc[:], T.srow[0:1, :], 128).then_inc(sem.selb, 1)
+        Y.wait_ge(sem.hsel, 7)
+        Y.wait_ge(sem.ldown, 16)
+        Y.dma_start(T.wrow[0:1, :], T.land[:, r // 2, :]).then_inc(sem.ldwish, 16)
+    else:
+        g.wait_ge(sem.sfd, 1)
     for items in CFG["sel"]:
         call = []
         for c, road, es in items:
-            for i, d in enumerate([partner] if c == "O" else to[c][:1] if road else to[c]):
-                e, a = p[es] if c == "O" or road else p[es][i::2], plans[d]["O"][0]
-                call.append(tx(topo, p[road] if road else cores[d], e, sem.hs if road else sem["sel" + c], T.sf[:, a:a + 2],
-                               T.selv[:, 2 * r:2 * r + 2]))
-                sent += len(e)
+            d = knows(plans, r, c)
+            a = min(plans[d]["O"])
+            call.append(tx(topo, p[road] if road else cores[d], p[es], sem.hsel if road else sem["sel" + c], T.sf[:, a:a + 2],
+                           T.selv[:, 2 * r:2 * r + 2]))
+            sent += len(p[es])
         g.remote_dma_fused(call, local_sem=sem.sent)
-    arrive = {c: len(p["off" if road else es]) for items in CFG["sel"] for c, road, es in items}
-
-    def picked(c):
-        return [partner] if c == "O" and idma else p[c]
-
-    def offs(c):
-        V.wait_ge(sem["sel" + c], arrive[c])
-        for d in picked(c):
-            a = 2 * d + p["O"].index(r)
-            col = T.sf[:, r:r + 1] if d == r else T.selv[:, a:a + 1]
-            V.tensor_scalar(T.wo[:, 32 * wpos[d]:32 * wpos[d] + 32], T.base[:], col, None, A.add).then_inc(sem["wo" + c], 1)
+    arrive = {}
+    for c, road, es in [x for items in CFG["sel"] for x in items]:
+        for n in ([c + "0", c + "1"] if c in "PQS" else [c]):
+            arrive[n] = len(p["off"]) // len(p[c]) if road else len(p[es])
 
     def places():
         first = float(CAPP * p["start"])
+        ix = [T.ix[0:16, 32 * k:32 * k + 32] for k in range(4)]
         V.wait_ge(sem.ldi, 32)
-        V.tensor_scalar(T.i0[0:16, :], T.pl[0:16, :], first, float(SLOTS), A.is_lt, A.mult).then_inc(sem.ix1, 1)
-        V.tensor_scalar(T.i1[0:16, :], T.ofl[0:16, :], float(SLOTS), first, A.mult, A.subtract).then_inc(sem.ix1, 1)
-        V.wait_ge(sem.ix1, 2)
-        V.tensor_tensor(T.i2[0:16, :], T.i0[0:16, :], T.pl[0:16, :], A.add).then_inc(sem.ix2, 1)
+        V.tensor_scalar(ix[0], T.pl[0:16, :], first, float(SLOTS), A.is_lt, A.mult).then_inc(sem.ix0, 1)
+        V.tensor_scalar(ix[1], T.ofl[0:16, :], float(SLOTS), first, A.mult, A.subtract).then_inc(sem.ix0, 1)
+        V.wait_ge(sem.ix0, 2)
+        V.tensor_tensor(ix[2], ix[0], T.pl[0:16, :], A.add).then_inc(sem.ix1, 1)
+        V.wait_ge(sem.ix1, 1)
+        V.tensor_tensor(ix[3], ix[1], ix[2], A.add).then_inc(sem.ix2, 1)
         V.wait_ge(sem.ix2, 1)
-        V.tensor_tensor(T.i3[0:16, :], T.i2[0:16, :], T.i1[0:16, :], A.add).then_inc(sem.ix4, 1)
-        V.wait_ge(sem.ix4, 1)
-        V.tensor_copy(T.idx[0:16, :], T.i3[0:16, :]).then_inc(sem.ix3, 1)
-        Y.wait_ge(sem.ix3, 1)
+        V.tensor_copy(T.idx[0:16, :], ix[3]).then_inc(sem.idx, 1)
+        Y.wait_ge(sem.idx, 1)
         for k in range(1, 8):
             Y.dma_start(T.idx[16 * k:16 * k + 16, :], T.idx[0:16, :]).then_inc(sem.rep, 16)
 
-    o0 = 0 if p["x0"] else SLOTS - CAPP
+    def pick(q, lo, hi, s):
+        out, win = T.wg[:, lo:hi], T.wt[:].indirect(T.wo[:, lo // 16:hi // 16])
+        (V.tensor_copy(out, win) if q is V else S.activation(out, win, COPY)).then_inc(s, 1)
+
+    o0 = 0 if p["first"] else SLOTS - CAPP
+    if CFG["places"] == "first":
+        places()
     for q in (V, S):
         q.wait_ge(sem.ldx, 32)
         q.wait_ge(sem.xo, len(runs))
-    V.wait_ge(sem.bas, 1)
-    if CFG["places"] == "first":
-        places()
-    for m, nxt in zip(make, make[1:] + [None]):
-        kind, c = m[0], m[1]
-        s = sem[kind + "g" + c]
+    own_end = 4 * NE * (pos["w"][r] + 1)
+    pending = None
+    for k, (kind, ns, share) in enumerate(make):
+        ds = [d for n in ns for d in p[n]]
+        s = sem["got%d" % k]
+        nxt = make[k + 1] if k + 1 < len(make) else ("", [], 0)
+        late = k + 1 in CFG["late"]
+        if kind == "x" and share < 0:
+            a = CAPP * pos["x"][ds[0]]
+            e = a + CAPP * len(ds)
+            for t in range(4):
+                S.activation(T.xg[:, 4 * a + t:4 * e:4], T.xt[:, t:4 * TC].indirect(T.xo[:, a // 16:e // 16]), COPY).then_inc(s, 1)
+            offs(nxt[1], sem["wo%d" % (k + 1)])
+            pending = (k, a, e)
+            continue
         if kind == "x":
-            a = CAPP * min(pos[d] for d in p[c])
-            e = a + 2 * CAPP * len(m[1:])
-            cut = a + CFG["vt"][c]
-            parts = [(V, a, e, 0), (V, a, cut, 1), (S, a, e, 2), (S, a, e, 3), (S, cut, e, 1)]
-            parts = [x for x in parts if x[1] < x[2]]
+            a = CAPP * pos["x"][ds[0]]
+            e, cut = a + CAPP * len(ds), a + share
+            parts = [x for x in [(V, a, e, 0), (V, a, cut, 1), (S, a, e, 2), (S, a, e, 3), (S, cut, e, 1)] if x[1] < x[2]]
             for q, lo, hi, t in parts:
                 out, win = T.xg[:, 4 * lo + t:4 * hi:4], T.xt[:, t:4 * TC].indirect(T.xo[:, lo // 16:hi // 16])
                 (V.tensor_copy(out, win) if q is V else S.activation(out, win, COPY)).then_inc(s, 1)
-            if nxt[0] == "w" and CFG["early"]:
-                offs(nxt[1])
+        else:
+            a = 4 * NE * pos["w"][ds[0]]
+            e = a + 4 * NE * len(ds)
+            parts = [x for x in [(S, a + share, e - pre * (r in ds)), (V, a, a + share)] if x[1] < x[2]]
+            if k + 1 in CFG["ahead"]:
+                offs([n for n in nxt[1] if n != "r"], sem["wo%d" % (k + 1)])
+            for q, lo, hi in parts:
+                q.wait_ge(sem.ldw, 32)
+                q.wait_ge(sem.own, 1)
+                if ns != ["r"]:
+                    q.wait_ge(sem["wo%d" % k], len(ds) - (r in ds))
+                pick(q, lo, hi, s)
+        if pending:
+            V.wait_ge(sem["got%d" % pending[0]], 4)
+            V.quantize_mx(T.xr[:, o0:o0 + 2 * CAPP], T.xrs[:, o0:o0 + 2 * CAPP], T.xg[:, 4 * pending[1]:4 * pending[2]]
+                          ).then_inc(sem["made%d" % pending[0]], 1)
+            pending = None
+        if nxt[0] == "w" and not late and k + 1 not in CFG["ahead"]:
+            offs([n for n in nxt[1] if n != "r"], sem["wo%d" % (k + 1)])
+        if parts:
             V.wait_ge(s, len(parts))
-            for c in m[1:]:
-                codes, plane, b = (T.xr, T.xrs, o0) if c == "O" else (T.xq, T.xs, a)
-                V.quantize_mx(codes[:, b:b + 2 * CAPP], plane[:, b:b + 2 * CAPP], T.xg[:, 4 * a:4 * (a + 2 * CAPP)]).then_inc(sem["x" + c], 1)
-                a += 2 * CAPP
-            if nxt[0] == "w" and not CFG["early"]:
-                offs(nxt[1])
-            continue
-        n = len(picked(c))
-        a = 4 * NE * wpos[picked(c)[0]]
-        mid, e = a + CFG["share"][c], a + 4 * NE * n
-        for q in (S, V):
-            q.wait_ge(sem.ldw, 32)
-            q.wait_ge(sem["wo" + c], n)
-        S.activation(T.wg[:, mid:e], T.wt[:].indirect(T.wo[:, mid // 16:e // 16]), COPY).then_inc(s, 1)
-        V.tensor_copy(T.wg[:, a:mid], T.wt[:].indirect(T.wo[:, a // 16:mid // 16])).then_inc(s, 1)
-        if nxt and nxt[1] not in CFG["late"]:
-            offs(nxt[1])
-        if m == CFG["places"]:
-            places()
-        V.wait_ge(s, 2)
-        V.quantize_mx(T.wq[:, a // 4:e // 4], T.ws[:, a // 4:e // 4], T.wg[:, a:e]).then_inc(sem[m], 1)
-        if nxt and nxt[1] in CFG["late"]:
-            offs(nxt[1])
-        if m == CFG["ownq"] and idma:
-            a = NE * wpos[r]
-            V.wait_ge(sem.idr, 16)
-            V.quantize_mx(T.wq[:, a:a + NE], T.ws[:, a:a + NE], T.wg[:, 4 * a:4 * (a + NE)]).then_inc(sem.wr, 1)
+        if kind == "w":
+            if pre and r in ds:
+                V.wait_ge(sem.pre, 1)
+            V.quantize_mx(T.wq[:, a // 4:e // 4], T.ws[:, a // 4:e // 4], T.wg[:, a:e]).then_inc(sem["made%d" % k], 1)
+        else:
+            far = e - CAPP * (r in ds)
+            V.quantize_mx(T.xq[:, a:far], T.xs[:, a:far], T.xg[:, 4 * a:4 * far]).then_inc(sem["made%d" % k], 1)
+            if far < e and not CFG["ownlate"]:
+                V.quantize_mx(T.xr[:, 0:NE], T.xrs[:, 0:NE], T.xg[:, 4 * (e - NE):4 * e]).then_inc(sem.xown, 1)
+        if k == CFG["ownlate"] and k:
+            V.quantize_mx(T.xr[:, 0:NE], T.xrs[:, 0:NE], T.xg[:, 4 * (SLOTS - NE):4 * SLOTS]).then_inc(sem.xown, 1)
+        if nxt[0] == "w" and late:
+            offs([n for n in nxt[1] if n != "r"], sem["wo%d" % (k + 1)])
+        if nxt[0] == "w" and all(m[0] == "x" for m in make[:k + 1]):
+            if pre:
+                S.wait_ge(sem.ldw, 32)
+                S.wait_ge(sem.own, 1)
+                pick(S, own_end - pre, own_end, sem.pre)
     if CFG["places"] == "last":
         places()
+    made = {k: 1 for k in range(len(make))}
 
-    js = jobs()
-    for k, (ready, _) in enumerate(CFG["steps"]):
-        if ready == "own":
-            a = 4 * NE * wpos[r]
-            g.wait_ge(sem.row, 1)
-            g.indirect_dma_start(T.wg[:, a:a + 4 * NE], None, T.w[:], IndirectOffsetOnAxis(ap=T.row[:], axis=0),
-                                 bounds_check=2 * NE - 1).then_inc(sem.idr, 16)
-            continue
-        for c in ready[1:]:
-            g.wait_ge(sem[ready[0] + c], 1)
-        kind = ready[0]
-        for i in (0, 1):
+    js = jobs(p)
+    for k, (m, _) in enumerate(CFG["steps"]):
+        if CFG["dsel"] and k == CFG["dsel"]:
+            g.wait_ge(sem.ldwish, 16)
+            g.partition_broadcast(T.wbc[:], T.wrow[0:1, :], 128).then_inc(sem.wbc, 1)
+        g.wait_ge(sem["made%d" % m], made[m])
+        for i in turn(p, k):
             call = []
-            for _, _, _, ranks, road, es, h in [j for j in js if j[0] == k and j[2] == i]:
+            for _, _, kind, _, ranks, road, es in [j for j in js if j[0] == k and j[3] == i]:
                 ds = p[ranks]
-                if kind == "x" and ranks == "o":
-                    src, a, w = (T.xr, T.xrs)[i], (0 if p["x0"] else SLOTS), CAPP
-                elif kind == "x":
-                    src, a, w = (T.xq, T.xs)[i], CAPP * pos[ds[0]], CAPP * len(ds)
-                else:
-                    src, a, w = (T.wq, T.ws)[i], NE * wpos[ds[0]], NE * len(ds)
+                a, w = WIDTH[kind] * pos[kind][ds[0]], WIDTH[kind] * len(ds)
+                src = ((T.xq, T.xs) if kind == "x" else (T.wq, T.ws))[i]
                 if road is None:
                     at = landing(T, plans, kind, r, ds[0])
-                    call.append(tx(topo, cores[ds[0]], p[es], at[2], src[:, a:a + w], at[i]))
+                    call.append(tx(topo, cores[ds[0]], p[es], sem[at[2]], src[:, a:a + w], at[i]))
                 else:
-                    call.append(tx(topo, p[road], p[es], sem["%s%d" % (h, i)], src[:, a:a + w], T[h + ("s" if i else "")][:, 0:w]))
+                    call.append(tx(topo, p[road], p[es], sem[("hc%d", "hp%d")[i] % k], src[:, a:a + w], T[("h%d", "hs%d")[i] % k][:, 0:w]))
                 sent += len(p[es])
             g.remote_dma_fused(call, local_sem=sem.sent)
     g.wait_ge(sem.sent, sent)
 
     come = {}
     for s in range(N):
-        for _, ready, i, ranks, road, es, _ in js:
+        for _, _, kind, i, ranks, road, es in js:
             if r in plans[s][ranks]:
-                key = "xin" if ready[0] == "x" else "we%d" % s
-                come[key] = come.get(key, 0) + last_hop(plans[s], ranks, road, es)
-    PE.wait_ge(sem.xin, come["xin"])
-    PE.wait_ge(sem.xO, 1)
-    for j, c in enumerate(CFG["todo"].split()):
-        h = [s for s in range(N) if r in plans[s][c]][0]
-        if h == r:
-            PE.wait_ge(sem.wr if idma else sem.wO, 1)
-            st, ss = T.wq[:, NE * wpos[r]:NE * (wpos[r] + 1)], T.ws[:, NE * wpos[r]:NE * (wpos[r] + 1)]
-        else:
+                key = landing(T, plans, kind, s, r)[2]
+                come[key] = come.get(key, 0) + len(last_hop(plans[s], ranks, road, es, r))
+    near = SLOTS - BANK
+    cols = {"a": (0, SLOTS // 2), "b": (SLOTS // 2, SLOTS), "E": (near, SLOTS) if p["first"] else (0, BANK),
+            "L": (0, near) if p["first"] else (BANK, SLOTS)}
+    step = {n: k for k, (kind, ns, _) in enumerate(make) for n in ns if n == "r" and kind == "w"}
+    tasks = CFG["todo"].split()
+    load = [0, 0]
+    PE.wait_ge(sem.xfar, come["xfar"])
+    for k, task in enumerate(tasks):
+        h, (lo, hi) = knows(plans, r, task[:-1]), cols[task[-1]]
+        if task[-1] != "E":
+            PE.wait_ge(sem.xnear, come["xnear"])
+            PE.wait_ge(sem.xown, 1)
+        if h != r:
             PE.wait_ge(sem["we%d" % h], come["we%d" % h])
-            st, ss = T.ew[:, NE * h:NE * (h + 1)], T.es[:, NE * h:NE * (h + 1)]
-        for i in (0, 1):
-            k = 2 * j + i
-            if k >= 8:
-                PE.wait_ge(sem["cp%d" % (k - 8)], 1)
-            x0, bank, out = p["x0"] + HALF * i, T.ps[:, 512 * (k % 8):512 * (k % 8) + HALF], SLOTS * h + HALF * i
-            PE.matmul_mx(bank, st, ss, T.xr[:, x0:x0 + HALF], T.xrs[:, x0:x0 + HALF], True, True).then_inc(sem["mm%d" % k], 1)
-            q, o = (S if i else V), T.res[:, out:out + HALF]
-            q.wait_ge(sem["mm%d" % k], 1)
-            (S.activation(o, bank, COPY) if i else V.tensor_copy(o, bank)).then_inc(sem["cp%d" % k] if k < 8 else sem.cpl, 1)
+            st, ss, a = T.ew, T.es, NE * h
+        else:
+            PE.wait_ge(sem["made%d" % step["r"]], 1)
+            st, ss, a = T.wq, T.ws, NE * pos["w"][r]
+        if k >= 8:
+            PE.wait_ge(sem["cp%d" % (k - 8)], 1)
+        x0, bank = p["x0"], T.ps[:, BANK * (k % 8):BANK * (k % 8) + hi - lo]
+        PE.matmul_mx(bank, st[:, a:a + NE], ss[:, a:a + NE], T.xr[:, x0 + lo:x0 + hi], T.xrs[:, x0 + lo:x0 + hi], True, True
+                     ).then_inc(sem["mm%d" % k], 1)
+        i = int(load[1] < load[0])
+        load[i] += hi - lo
+        q, o = (V, S)[i ^ CFG.get("flip", 0)], T.res[:, SLOTS * h + lo:SLOTS * h + hi]
+        q.wait_ge(sem["mm%d" % k], 1)
+        (V.tensor_copy(o, bank) if q is V else S.activation(o, bank, COPY)).then_inc(sem["cp%d" % k] if k < 8 else sem.cpl, 1)
 
     h = TC // 2
     for q in (V, S):
         q.wait_ge(sem.rep, 112)
-        q.wait_ge(sem.ix3, 1)
+        q.wait_ge(sem.idx, 1)
         q.wait_ge(sem.cpl, 8)
-    V.tensor_copy(T.yt[:, 0:h], T.res[:].indirect(T.idx[:, 0:16])).then_inc(sem.gv, 1)
-    S.activation(T.yt[:, h:TC], T.res[:].indirect(T.idx[:, 16:32]), COPY).then_inc(sem.gs, 1)
-    Y.wait_ge(sem.gv, 1)
-    Y.wait_ge(sem.gs, 1)
-    Y.dma_start(T.y[:], T.yt[:]).then_inc(sem.yd, 16)
-    Y.wait_ge(sem.yd, 16)
+    a = 0
+    for k, n in enumerate(CFG["out"]):
+        s = (sem.gv, sem.gs)[k]
+        V.tensor_copy(T.yt[:, a:a + n], T.res[:].indirect(T.idx[:, a // 16:(a + n) // 16])).then_inc(s, 1)
+        S.activation(T.yt[:, a + n:a + 2 * n], T.res[:].indirect(T.idx[:, (a + n) // 16:(a + 2 * n) // 16]), COPY).then_inc(s, 1)
+        Y.wait_ge(s, 2)
+        Y.dma_start(T.y[:, a:a + 2 * n], T.yt[:, a:a + 2 * n]).then_inc(sem.yd, 16)
+        a += 2 * n
+    Y.wait_ge(sem.yd, 16 * len(CFG["out"]))

from concourse.bass import DstId, RemoteDMATransfer
from concourse.mybir import dt, AluOpType, ActivationFunctionType

N, TC, CAPP, NE = 8, 512, 96, 128
SLOTS = N * CAPP
BANK = 512
CODE = "float8_e4m3fn_x4"
NAMES = ["Q0", "Q1", "S0", "S1", "P0", "P1", "o", "r"]

CFG = {
    "make": [("x", "P S", 384), ("x", "Q1 Q0 o r", 256), ("w", "Q0 Q1", 512), ("w", "S0 P0", 448), ("w", "S1 P1", 448),
             ("w", "o r", 320)],
    "pre": 256, "places": "last", "flip": 0, "late": [2], "dsel": 0, "ownlate": 2, "ahead": [5], "out": [128, 128], "head": 32,
    "stagger": range(N),
    "steps": [
        (0, [("P", "F0", "F1", "off"), ("S", "B", "C", "on")]),
        (1, [("Q0+o", "A", "A", "on")]),
        (1, [("Q1", None, None, "off")]),
        (2, [("Q0", "A", "A", "on"), ("Q1", None, None, "off")]),
        (3, [("S0", "B", "B", "on"), ("P0", None, None, "off")]),
        (4, [("S1", "B", "B", "on"), ("P1", None, None, "off")]),
        (5, [("o", None, None, "on")]),
    ],
    "sel": [[("Q0", None, "off0"), ("Q1", None, "off1"), ("S1", "B", "on0"), ("P1", "A", "on1")],
            [("S0", None, "off0"), ("P0", None, "off1"), ("o", None, "on0")]],
    "todo": "Q1a Q1b ra rb P0a P0b Q0a Q0b S0a S0b oa ob P1a P1b S1a S1b",
}


def sb(n, t, p=128):
    return ("sbuf", [p, n], t)


SCRATCH = {
    "srow": sb(16, "int32", 1), "sbc": sb(16, "int32"), "sf": sb(16, "bfloat16"), "selv": sb(2 * N, "bfloat16"),
    "sd": ("dram", [128, 2], "int32"), "land": ("dram", [N, 128, 2], "int32"), "wrow": sb(16, "int32", 1), "wbc": sb(16, "int32"),
    "snd": sb(SLOTS // 16, "int32"), "xo": sb(SLOTS // 16, "uint16"),
    "ip": sb(32, "int32"), "ia": sb(32, "int32"), "ic": sb(32, "int32"), "base": sb(32, "float32"), "wo": sb(32 * N, "uint16"),
    "pl": sb(32, "int32"), "ofl": sb(32, "int32"), "ix": sb(32 * 4, "float32"), "idx": sb(32, "uint16"),
    "xt": sb(4 * TC, "bfloat16"), "xg": sb(4 * SLOTS, "bfloat16"), "xq": sb(SLOTS, CODE), "xs": sb(SLOTS, "uint8"),
    "wt": sb(8 * NE, "bfloat16"), "wg": sb(4 * NE * N, "bfloat16"), "wq": sb(NE * N, CODE), "ws": sb(NE * N, "uint8"),
    "xr": sb(SLOTS + CAPP, CODE), "xrs": sb(SLOTS + CAPP, "uint8"), "ew": sb(NE * N, CODE), "es": sb(NE * N, "uint8"),
    **{"h%d" % k: sb(3 * NE, CODE) for k in range(N + 1)}, **{"hs%d" % k: sb(3 * NE, "uint8") for k in range(N + 1)},
    "ps": ("psum", [128, 4096], "float32"), "res": sb(N * SLOTS, "float32"), "yt": sb(TC, "float32"),
}
SEMAPHORES = (["ldsel", "ldsnd", "ldx", "ldw", "ldi", "rep", "yd", "iot", "ian", "bas", "selb", "sfd", "xo", "own", "pre", "xown", "ldsd", "ldown", "ldwish", "wbc", "wf",
               "idx", "xfar", "xnear", "cpl", "gv", "gs", "sent", "hsel", "ix0", "ix1", "ix2"] + ["sel" + n for n in NAMES]
              + [a + "%d" % k for a in ("we", "cp", "wo", "got", "made", "hc", "hp") for k in range(N + 1)] + ["mm%d" % k for k in range(2 * N)])
WIDTH = {"x": CAPP, "w": NE}


def bits(es):
    m = 0
    for e in es:
        m |= 1 << e
    return m


def plan(r, T, topo):
    cores = list(T.cores)
    core = cores[r]
    chips = []
    for c in cores:
        if topo.chip(c) not in chips:
            chips.append(topo.chip(c))
    pair = [[d for d in range(N) if topo.chip(cores[d]) == h] for h in chips]
    k = chips.index(topo.chip(core))
    rest = [(k + i) % len(chips) for i in range(1, len(chips))]
    same = [i for i in rest if topo.same_plane(chips[i], chips[k])]
    cross = [i for i in rest if i not in same]
    p = {"O": pair[k][::-1], "S": pair[same[0]], "P": pair[cross[0]], "Q": pair[cross[1]]}
    mine = pair[k].index(r)
    p["o"], p["r"] = [pair[k][1 - mine]], [r]
    for c in "QSP":
        p[c + "0"], p[c + "1"] = [p[c][mine]], [p[c][1 - mine]]
    free = [c for c in topo.cores_of(core) if c not in cores]
    away = [c for c in free if topo.die(c) != topo.die(core)]
    owners = [c for c in away if all(topo.may_write(c, cores[d]) for d in p["Q"])]
    p["A"] = owners[mine]
    p["B"] = [c for c in away if c not in owners][mine]
    p["C"] = [c for c in free if c not in away][mine]
    far = cores[p["P"][0]]
    doors = [c for c in range(topo.CHIPS * topo.CORES_PER_CHIP) if topo.mates(topo.chip(c), topo.chip(far)) and topo.may_write(c, far)]
    p["F0"], p["F1"] = doors[mine::2]
    far2 = cores[p["Q"][0]]
    doors = [c for c in range(topo.CHIPS * topo.CORES_PER_CHIP) if topo.mates(topo.chip(c), topo.chip(far2)) and topo.may_write(c, far2)]
    p["G0"], p["G1"] = doors[mine::2]
    off = topo.engines(core, far)
    on = [e for e in topo.engines(core, cores[p["o"][0]]) if e not in off]
    for n, es in (("off", off), ("on", on)):
        h = len(es) // 2
        p[n], p[n + "0"], p[n + "1"] = es, es[:h], es[h:]
        p[n + "2"], p[n + "3"] = es[h:h + h // 2], es[h + h // 2:]
    p["all"] = off + on
    p["a0"], p["a1"] = off[0:2], off[2:4]
    p["first"] = mine == 0
    p["start"] = r
    p["x0"] = NE - CAPP
    for _, items in CFG["steps"]:
        for ns, *_ in items:
            p[ns] = [d for n in ns.split("+") for d in p[n]]
    return p


def knows(plans, r, name):
    return [s for s in range(N) if r in plans[s][name]][0]


def tx(topo, c, es, rs, src, dst):
    rid, pid, _ = topo.addr(c)
    if src.dtype == dt.float8_e4m3fn_x4:
        src, dst = src.bitcast(dt.uint8), dst.bitcast(dt.uint8)
    return RemoteDMATransfer(dst_ids=[DstId(rid=rid, pnc=pid)], dma_engine_mask=bits(es), remote_sem=rs, src=src, dst=dst)


def landing(T, plans, kind, s, d):
    if kind == "x":
        a = plans[d]["x0"] + CAPP * ((s - plans[d]["start"]) % N)
        return T.xr[:, a:a + CAPP], T.xrs[:, a:a + CAPP], "xnear" if s in plans[d]["O"] else "xfar"
    return T.ew[:, NE * s:NE * (s + 1)], T.es[:, NE * s:NE * (s + 1)], "we%d" % s


def last_hop(p, ranks, road, es, d):
    if road is None:
        return p[es]
    if d in p["o"]:
        return p["on"]
    far = [x for x in p[ranks] if x not in p["o"]]
    n = len(p["off"]) // len(far)
    return p["off"][n * far.index(d):n * far.index(d) + n]


def jobs(p):
    return [(k, m, CFG["make"][m][0], i, ranks, road[i], es) for k, (m, items) in enumerate(CFG["steps"])
            for i in turn(p, k) for ranks, *road, es in items]


def turn(p, k):
    return (0, 1) if p["first"] or k not in CFG["stagger"] else (1, 0)


def helper_program(g, core, T, topo, plans):
    sent = 0
    for r, p in enumerate(plans):
        for c, road, es in [x for items in CFG["sel"] for x in items if x[1] and p[x[1]] == core]:
            g.wait_ge(T.sem.hsel, len(p[es]))
            ns = [c + "0", c + "1"] if c in "PQS" else [c]
            n, two = len(p["off"]) // len(ns), T.selv[:, 2 * r:2 * r + 2]
            g.remote_dma_fused([tx(topo, T.cores[knows(plans, r, x)], p["off"][j * n:j * n + n], T.sem["sel" + x], two, two)
                                for j, x in enumerate(ns)], local_sem=T.sem.sent)
            sent += len(p["off"])
        for k, _, kind, i, ranks, road, es in jobs(p):
            if road is None or p[road] != core:
                continue
            w, src = WIDTH[kind], T[("h%d", "hs%d")[i] % k]
            g.wait_ge(T.sem[("hc%d", "hp%d")[i] % k], len(p[es]))
            call = []
            for j, d in enumerate(p[ranks]):
                to, by = landing(T, plans, kind, r, d), last_hop(p, ranks, road, es, d)
                call.append(tx(topo, T.cores[d], by, T.sem[to[2]], src[:, j * w:(j + 1) * w], to[i]))
                sent += len(by)
            g.remote_dma_fused(call, local_sem=T.sem.sent)
    if sent:
        g.wait_ge(T.sem.sent, sent)


def rank_program(g, core, T, topo):
    plans = [plan(r, T, topo) for r in range(N)]
    r = T.rank_of(core)
    if r is None:
        return helper_program(g, core, T, topo, plans)
    V, S, PE, Y = g.vector, g.scalar, g.tensor, g.sync
    sem, A = T.sem, AluOpType
    COPY = ActivationFunctionType.Copy
    cores = T.cores
    p = plans[r]
    make = [(kind, ns.split(), share) for kind, ns, share in CFG["make"]]
    pos = {kind: {d: k for k, d in enumerate(d for a, ns, _ in make if a == kind for n in ns for d in p[n])} for kind in "xw"}
    name = {p[n][0]: n for n in NAMES}
    pre = CFG["pre"]
    got = []

    def lists():
        S.dma_start(T.ofl[0:16, :], T.of[:]).then_inc(sem.ldi, 16)
        Y.dma_start(T.pl[0:16, :], T.place[:]).then_inc(sem.ldi, 16)

    if CFG["dsel"]:
        Y.dma_start(T.sd[0:8, :], T.sel[:]).then_inc(sem.ldsd, 16)
    (S if CFG["dsel"] else Y).dma_start(T.srow[0:1, :], T.sel[:]).then_inc(sem.ldsel, 16)
    cut = CFG["head"] or 64
    if CFG["head"]:
        S.dma_start(T.xt[0:cut, :], T.x[0:cut, :]).then_inc(sem.ldx, 16)
    for k in range(8):
        (Y if k % 2 else S).dma_start(T.snd[16 * k:16 * k + 16, :], T.send[:]).then_inc(sem.ldsnd, 16)
    if CFG["places"] == "first":
        lists()
    if not CFG["head"]:
        S.dma_start(T.xt[0:cut, :], T.x[0:cut, :]).then_inc(sem.ldx, 16)
    Y.dma_start(T.xt[cut:128, :], T.x[cut:128, :]).then_inc(sem.ldx, 16)
    if CFG["places"] != "first":
        lists()
    Y.dma_start(T.wt[:, 4 * NE:8 * NE], T.w[128:256, :]).then_inc(sem.ldw, 16)
    Y.dma_start(T.wt[:, 0:4 * NE], T.w[0:128, :]).then_inc(sem.ldw, 16)
    if CFG["dsel"]:
        S.dma_start(T.land[r, 0:8, :], T.sel[:]).then_inc(sem.ldown, 16)

    g.iota(T.ip[:], [[0, 32]], 0, 1).then_inc(sem.iot, 1)
    g.iota(T.ic[:], [[16, 32]], 0, 0).then_inc(sem.iot, 1)
    if CFG["dsel"]:
        g.wait_ge(sem.ldsd, 16)
    else:
        g.wait_ge(sem.ldsel, 16)
        g.partition_broadcast(T.sbc[:], T.srow[0:1, :], 128).then_inc(sem.selb, 1)

    def offs(ns, s):
        for d in [d for n in ns for d in p[n]]:
            if d != r and CFG["dsel"]:
                if not got:
                    V.wait_ge(sem.wbc, 1)
                    V.tensor_scalar(T.selv[:], T.wbc[:], float(4 * NE), 0.0, A.mult, A.max).then_inc(sem.wf, 1)
                    V.wait_ge(sem.wf, 1)
                    got.append(1)
            elif d != r:
                V.wait_ge(sem["sel" + name[d]], arrive[name[d]])
            b = 2 * d + r - min(p["O"])
            a, col = 32 * pos["w"][d], T.sf[:, r:r + 1] if d == r else T.selv[:, b:b + 1]
            V.tensor_scalar(T.wo[:, a:a + 32], T.base[:], col, None, A.add).then_inc(s, 1)

    V.wait_ge(sem.iot, 2)
    V.tensor_scalar(T.ia[:], T.ip[:], 15, None, A.bitwise_and).then_inc(sem.ian, 1)
    V.wait_ge(sem.ian, 1)
    V.tensor_tensor(T.base[:], T.ia[:], T.ic[:], A.add).then_inc(sem.bas, 1)
    V.wait_ge(sem.selb, 1)
    V.tensor_scalar(T.sf[:], T.sbc[:], float(4 * NE), 0.0, A.mult, A.max).then_inc(sem.sfd, 1)
    V.wait_ge(sem.sfd, 1)
    V.wait_ge(sem.bas, 1)
    offs(["r"], sem.own)
    V.wait_ge(sem.ldsnd, 128)
    runs = []
    for d in pos["x"]:
        if runs and runs[-1][-1] + 1 == d:
            runs[-1].append(d)
        else:
            runs.append([d])
    for ds in runs:
        a, d, n = 6 * pos["x"][ds[0]], ds[0], 6 * len(ds)
        V.tensor_scalar(T.xo[:, a:a + n], T.snd[:, 6 * d:6 * d + n], 4.0, 0.0, A.mult, A.max).then_inc(sem.xo, 1)

    sent = 0
    if CFG["dsel"]:
        es = p["off"][:6] + p["on"][:1]
        others = [knows(plans, r, n) for n in NAMES[:7]]
        g.remote_dma_fused([tx(topo, cores[d], [e], sem.hsel, T.sd[:], T.land[r]) for d, e in zip(others, es)], local_sem=sem.sent)
        sent += 7
        g.wait_ge(sem.ldsel, 16)
        g.partition_broadcast(T.sbc[:], T.srow[0:1, :], 128).then_inc(sem.selb, 1)
        Y.wait_ge(sem.hsel, 7)
        Y.wait_ge(sem.ldown, 16)
        Y.dma_start(T.wrow[0:1, :], T.land[:, r // 2, :]).then_inc(sem.ldwish, 16)
    else:
        g.wait_ge(sem.sfd, 1)
    for items in CFG["sel"]:
        call = []
        for c, road, es in items:
            d = knows(plans, r, c)
            a = min(plans[d]["O"])
            call.append(tx(topo, p[road] if road else cores[d], p[es], sem.hsel if road else sem["sel" + c], T.sf[:, a:a + 2],
                           T.selv[:, 2 * r:2 * r + 2]))
            sent += len(p[es])
        g.remote_dma_fused(call, local_sem=sem.sent)
    arrive = {}
    for c, road, es in [x for items in CFG["sel"] for x in items]:
        for n in ([c + "0", c + "1"] if c in "PQS" else [c]):
            arrive[n] = len(p["off"]) // len(p[c]) if road else len(p[es])

    def places():
        first = float(CAPP * p["start"])
        ix = [T.ix[0:16, 32 * k:32 * k + 32] for k in range(4)]
        V.wait_ge(sem.ldi, 32)
        V.tensor_scalar(ix[0], T.pl[0:16, :], first, float(SLOTS), A.is_lt, A.mult).then_inc(sem.ix0, 1)
        V.tensor_scalar(ix[1], T.ofl[0:16, :], float(SLOTS), first, A.mult, A.subtract).then_inc(sem.ix0, 1)
        V.wait_ge(sem.ix0, 2)
        V.tensor_tensor(ix[2], ix[0], T.pl[0:16, :], A.add).then_inc(sem.ix1, 1)
        V.wait_ge(sem.ix1, 1)
        V.tensor_tensor(ix[3], ix[1], ix[2], A.add).then_inc(sem.ix2, 1)
        V.wait_ge(sem.ix2, 1)
        V.tensor_copy(T.idx[0:16, :], ix[3]).then_inc(sem.idx, 1)
        Y.wait_ge(sem.idx, 1)
        for k in range(1, 8):
            Y.dma_start(T.idx[16 * k:16 * k + 16, :], T.idx[0:16, :]).then_inc(sem.rep, 16)

    def pick(q, lo, hi, s):
        out, win = T.wg[:, lo:hi], T.wt[:].indirect(T.wo[:, lo // 16:hi // 16])
        (V.tensor_copy(out, win) if q is V else S.activation(out, win, COPY)).then_inc(s, 1)

    o0 = 0 if p["first"] else SLOTS - CAPP
    if CFG["places"] == "first":
        places()
    for q in (V, S):
        q.wait_ge(sem.ldx, 32)
        q.wait_ge(sem.xo, len(runs))
    own_end = 4 * NE * (pos["w"][r] + 1)
    pending = None
    for k, (kind, ns, share) in enumerate(make):
        ds = [d for n in ns for d in p[n]]
        s = sem["got%d" % k]
        nxt = make[k + 1] if k + 1 < len(make) else ("", [], 0)
        late = k + 1 in CFG["late"]
        if kind == "x" and share < 0:
            a = CAPP * pos["x"][ds[0]]
            e = a + CAPP * len(ds)
            for t in range(4):
                S.activation(T.xg[:, 4 * a + t:4 * e:4], T.xt[:, t:4 * TC].indirect(T.xo[:, a // 16:e // 16]), COPY).then_inc(s, 1)
            offs(nxt[1], sem["wo%d" % (k + 1)])
            pending = (k, a, e)
            continue
        if kind == "x":
            a = CAPP * pos["x"][ds[0]]
            e, cut = a + CAPP * len(ds), a + share
            parts = [x for x in [(V, a, e, 0), (V, a, cut, 1), (S, a, e, 2), (S, a, e, 3), (S, cut, e, 1)] if x[1] < x[2]]
            for q, lo, hi, t in parts:
                out, win = T.xg[:, 4 * lo + t:4 * hi:4], T.xt[:, t:4 * TC].indirect(T.xo[:, lo // 16:hi // 16])
                (V.tensor_copy(out, win) if q is V else S.activation(out, win, COPY)).then_inc(s, 1)
        else:
            a = 4 * NE * pos["w"][ds[0]]
            e = a + 4 * NE * len(ds)
            parts = [x for x in [(S, a + share, e - pre * (r in ds)), (V, a, a + share)] if x[1] < x[2]]
            if k + 1 in CFG["ahead"]:
                offs([n for n in nxt[1] if n != "r"], sem["wo%d" % (k + 1)])
            for q, lo, hi in parts:
                q.wait_ge(sem.ldw, 32)
                q.wait_ge(sem.own, 1)
                if ns != ["r"]:
                    q.wait_ge(sem["wo%d" % k], len(ds) - (r in ds))
                pick(q, lo, hi, s)
        if pending:
            V.wait_ge(sem["got%d" % pending[0]], 4)
            V.quantize_mx(T.xr[:, o0:o0 + 2 * CAPP], T.xrs[:, o0:o0 + 2 * CAPP], T.xg[:, 4 * pending[1]:4 * pending[2]]
                          ).then_inc(sem["made%d" % pending[0]], 1)
            pending = None
        if nxt[0] == "w" and not late and k + 1 not in CFG["ahead"]:
            offs([n for n in nxt[1] if n != "r"], sem["wo%d" % (k + 1)])
        if parts:
            V.wait_ge(s, len(parts))
        if kind == "w":
            if pre and r in ds:
                V.wait_ge(sem.pre, 1)
            V.quantize_mx(T.wq[:, a // 4:e // 4], T.ws[:, a // 4:e // 4], T.wg[:, a:e]).then_inc(sem["made%d" % k], 1)
        else:
            far = e - CAPP * (r in ds)
            V.quantize_mx(T.xq[:, a:far], T.xs[:, a:far], T.xg[:, 4 * a:4 * far]).then_inc(sem["made%d" % k], 1)
            if far < e and not CFG["ownlate"]:
                V.quantize_mx(T.xr[:, 0:NE], T.xrs[:, 0:NE], T.xg[:, 4 * (e - NE):4 * e]).then_inc(sem.xown, 1)
        if k == CFG["ownlate"] and k:
            V.quantize_mx(T.xr[:, 0:NE], T.xrs[:, 0:NE], T.xg[:, 4 * (SLOTS - NE):4 * SLOTS]).then_inc(sem.xown, 1)
        if nxt[0] == "w" and late:
            offs([n for n in nxt[1] if n != "r"], sem["wo%d" % (k + 1)])
        if nxt[0] == "w" and all(m[0] == "x" for m in make[:k + 1]):
            if pre:
                S.wait_ge(sem.ldw, 32)
                S.wait_ge(sem.own, 1)
                pick(S, own_end - pre, own_end, sem.pre)
    if CFG["places"] == "last":
        places()
    made = {k: 1 for k in range(len(make))}

    js = jobs(p)
    for k, (m, _) in enumerate(CFG["steps"]):
        if CFG["dsel"] and k == CFG["dsel"]:
            g.wait_ge(sem.ldwish, 16)
            g.partition_broadcast(T.wbc[:], T.wrow[0:1, :], 128).then_inc(sem.wbc, 1)
        g.wait_ge(sem["made%d" % m], made[m])
        for i in turn(p, k):
            call = []
            for _, _, kind, _, ranks, road, es in [j for j in js if j[0] == k and j[3] == i]:
                ds = p[ranks]
                a, w = WIDTH[kind] * pos[kind][ds[0]], WIDTH[kind] * len(ds)
                src = ((T.xq, T.xs) if kind == "x" else (T.wq, T.ws))[i]
                if road is None:
                    at = landing(T, plans, kind, r, ds[0])
                    call.append(tx(topo, cores[ds[0]], p[es], sem[at[2]], src[:, a:a + w], at[i]))
                else:
                    call.append(tx(topo, p[road], p[es], sem[("hc%d", "hp%d")[i] % k], src[:, a:a + w], T[("h%d", "hs%d")[i] % k][:, 0:w]))
                sent += len(p[es])
            g.remote_dma_fused(call, local_sem=sem.sent)
    g.wait_ge(sem.sent, sent)

    come = {}
    for s in range(N):
        for _, _, kind, i, ranks, road, es in js:
            if r in plans[s][ranks]:
                key = landing(T, plans, kind, s, r)[2]
                come[key] = come.get(key, 0) + len(last_hop(plans[s], ranks, road, es, r))
    near = SLOTS - BANK
    cols = {"a": (0, SLOTS // 2), "b": (SLOTS // 2, SLOTS), "E": (near, SLOTS) if p["first"] else (0, BANK),
            "L": (0, near) if p["first"] else (BANK, SLOTS)}
    step = {n: k for k, (kind, ns, _) in enumerate(make) for n in ns if n == "r" and kind == "w"}
    tasks = CFG["todo"].split()
    load = [0, 0]
    PE.wait_ge(sem.xfar, come["xfar"])
    for k, task in enumerate(tasks):
        h, (lo, hi) = knows(plans, r, task[:-1]), cols[task[-1]]
        if task[-1] != "E":
            PE.wait_ge(sem.xnear, come["xnear"])
            PE.wait_ge(sem.xown, 1)
        if h != r:
            PE.wait_ge(sem["we%d" % h], come["we%d" % h])
            st, ss, a = T.ew, T.es, NE * h
        else:
            PE.wait_ge(sem["made%d" % step["r"]], 1)
            st, ss, a = T.wq, T.ws, NE * pos["w"][r]
        if k >= 8:
            PE.wait_ge(sem["cp%d" % (k - 8)], 1)
        x0, bank = p["x0"], T.ps[:, BANK * (k % 8):BANK * (k % 8) + hi - lo]
        PE.matmul_mx(bank, st[:, a:a + NE], ss[:, a:a + NE], T.xr[:, x0 + lo:x0 + hi], T.xrs[:, x0 + lo:x0 + hi], True, True
                     ).then_inc(sem["mm%d" % k], 1)
        i = int(load[1] < load[0])
        load[i] += hi - lo
        q, o = (V, S)[i ^ CFG.get("flip", 0)], T.res[:, SLOTS * h + lo:SLOTS * h + hi]
        q.wait_ge(sem["mm%d" % k], 1)
        (V.tensor_copy(o, bank) if q is V else S.activation(o, bank, COPY)).then_inc(sem["cp%d" % k] if k < 8 else sem.cpl, 1)

    h = TC // 2
    for q in (V, S):
        q.wait_ge(sem.rep, 112)
        q.wait_ge(sem.idx, 1)
        q.wait_ge(sem.cpl, 8)
    a = 0
    for k, n in enumerate(CFG["out"]):
        s = (sem.gv, sem.gs)[k]
        V.tensor_copy(T.yt[:, a:a + n], T.res[:].indirect(T.idx[:, a // 16:(a + n) // 16])).then_inc(s, 1)
        S.activation(T.yt[:, a + n:a + 2 * n], T.res[:].indirect(T.idx[:, (a + n) // 16:(a + 2 * n) // 16]), COPY).then_inc(s, 1)
        Y.wait_ge(s, 2)
        Y.dma_start(T.y[:, a:a + 2 * n], T.yt[:, a:a + 2 * n]).then_inc(sem.yd, 16)
        a += 2 * n
    Y.wait_ge(sem.yd, 16 * len(CFG["out"]))
